import numpy as np
import ml_dtypes


def mxq(x, axis, fmt="e4m3"):
    dtype, down = {"e4m3": (ml_dtypes.float8_e4m3fn, 7), "e5m2": (ml_dtypes.float8_e5m2, 14)}[fmt]
    v = np.moveaxis(np.asarray(x, np.float32).astype(ml_dtypes.bfloat16).astype(np.float64), axis, -1)
    blocks = v.reshape(v.shape[:-1] + (-1, 32))
    amax = np.abs(blocks).max(-1, keepdims=True)
    byte = np.maximum(np.where(amax > 0, np.frexp(amax)[1] - 1 + 127, 0) - down, 1)
    scale = np.exp2(byte - 127.0)
    codes = (blocks / scale).astype(np.float32).astype(dtype).astype(np.float64)
    return np.moveaxis((codes * scale).reshape(v.shape), -1, axis)


WIDE = False


def mx_kscale(k):
    if not WIDE:
        return np.ones(k)
    levels = np.array([10, -10, 5, -5, 0])
    if k % 512:
        return np.exp2(np.random.permutation(np.resize(levels, k // 32))).repeat(32)
    a = np.empty((k // 512, 16))
    for p in range(k // 512):
        a[p, :8] = np.random.permutation(np.resize(levels, 8))
        for g in range(8):
            far = levels[np.abs(levels - a[p, g]) >= 10]
            a[p, g + 8] = far[np.random.randint(len(far))]
    return np.exp2(a.ravel()).repeat(32)


def f64(x):
    return np.asarray(x).astype(np.float64)


def striped(idx):
    return np.tile(idx.reshape(-1, 16).T, (8, 1)).astype(np.uint16)


def unstriped(offs):
    return offs[:16].T.reshape(-1).astype(np.int64)


def pack_weight(w):
    k, n = w.shape
    w = f64(np.asarray(w, np.float32).astype(ml_dtypes.bfloat16)).reshape(k // 32, 32, n)
    amax = np.abs(w).max(1)
    byte = np.clip(np.where(amax > 0, np.frexp(amax)[1] - 1 + 127 - 7, 1), 1, 254)
    scaled = (w * np.exp2(127.0 - byte)[:, None, :]).reshape(k, n).astype(np.float32)
    words = np.ascontiguousarray(scaled.reshape(k // 512, 128, 4, n).transpose(0, 1, 3, 2)).astype(ml_dtypes.float8_e4m3fn).view(np.uint8)
    return words, np.ascontiguousarray(byte.astype(np.uint8).reshape(k // 512, 16, n))


def unpack_weight(words, scales):
    g, p, n, _ = words.shape
    vals = np.ascontiguousarray(words).view(ml_dtypes.float8_e4m3fn).astype(np.float64) * np.repeat(np.exp2(scales.astype(np.float64) - 127.0), 8, axis=1)[..., None]
    return vals.transpose(0, 1, 3, 2).reshape(g * 512, n)


def planes(y):
    n, m = y.shape
    v = y.astype(np.float32).astype(ml_dtypes.bfloat16).astype(np.float64).reshape(n // 32, 32, m)
    top = np.abs(v).max(1)
    byte = np.clip(np.where(top > 0, np.frexp(top)[1] - 1 + 127 - 7, 1), 1, 254)
    codes = (v * np.exp2(127.0 - byte)[:, None, :]).reshape(n, m).astype(np.float32).astype(ml_dtypes.float8_e4m3fn).view(np.uint8)
    words = codes.reshape(n // 512, 128, 4, m).transpose(0, 1, 3, 2)
    return np.ascontiguousarray(words), np.ascontiguousarray(byte.astype(np.uint8).reshape(n // 512, 16, m))


K, T, S, N, U = 1024, 1024, 512, 512, 1024
P = 2 ** 7


def setup_inputs():
    n = np.random.standard_normal
    s = mx_kscale(K)[:, None]
    packed_xT = pack_weight(n((K, T)) * s)
    return {
        "x_words": packed_xT[0],
        "x_scales": packed_xT[1],
        "cache": (n((N, U))).astype(np.float32),
        "w1": (n((K, N)) / np.sqrt(K) / s).astype(np.float32),
        "scale": (np.tile(np.random.uniform(0.5, 1.5, S), (P, 1))).astype(np.float32),
        "offs": striped(np.random.permutation(T)[:S]),
        "slot": striped(np.random.permutation(U)[:S]),
    }


def reference(x_words, x_scales, cache, w1, scale, offs, slot):
    xq = unpack_weight(x_words, x_scales)[:, unstriped(offs)]
    y = mxq(f64(w1), 0, "e4m3").T @ xq
    r = np.tanh(y * f64(scale)[:1])
    out = f64(cache).copy()
    out[:, unstriped(slot)] = r
    out_0 = out
    return (out_0,) + planes(out_0)

@@ -1,0 +1,198 @@
+from contextlib import ExitStack
+
+import concourse.mybir as mybir
+from concourse.masks import make_identity
+
+K, T, S, N, U = 1024, 1024, 512, 512, 1024
+FLOPS = 2 * K * N * S
+
+F32 = mybir.dt.float32
+BF16 = mybir.dt.bfloat16
+I32 = mybir.dt.int32
+U32 = mybir.dt.uint32
+U16 = mybir.dt.uint16
+U8 = mybir.dt.uint8
+FP8X4 = mybir.dt.float8_e4m3fn_x4
+TANH = mybir.ActivationFunctionType.Tanh
+MULT = mybir.AluOpType.mult
+
+P = 128
+PACK = 4
+LIST_ROWS = 16
+BLOCKS = S // P
+ON_SCALAR = (64, 24, 32, 20)
+
+
+def tile_picked_zkvw_tanh_po_kernel(tc, x_words, x_scales, cache, w1, scale, offs, slot, out_0, out_1, out_2):
+    nc = tc.nc
+    with ExitStack() as ctx:
+        held = ctx.enter_context(tc.tile_pool(name="held", bufs=1))
+        psum = ctx.enter_context(tc.psum_pool(name="psum", bufs=1))
+
+        def sb(name, shape, dtype, tag=None):
+            return held.tile(shape, dtype, name=name, tag=tag or name, align_bytes=64)
+
+        def bank(name, index):
+            return psum.tile([P, 512], F32, name=name, tag="bank%d" % index)
+
+        offs_sb = sb("offs_sb", [P, S // LIST_ROWS], U16)
+        slot_sb = sb("slot_sb", [P, S // LIST_ROWS], U16)
+        xw = [sb("xw%d" % g, [P, T], U32) for g in range(2)]
+        xs = sb("xs", [P, T], U8)
+        w_raw = [[sb("w_raw%d_%d" % (g, h), [P, PACK, N // 2], F32) for h in range(2)] for g in range(2)]
+        scale_rows = sb("scale_rows", [P, P], F32)
+        scale_sb = sb("scale_sb", [P, S], F32)
+        window = [sb("window%d" % t, [P, U], F32) for t in range(PACK)]
+        ident = sb("ident", [P, P], F32)
+        warm = sb("warm", [P, 2], F32)
+
+        nc.gpsimd.memset(xs[:].bitcast(I32), 0)
+        make_identity(nc, ident[:])
+        nc.vector.memset(warm[:, 0:1], 0.0)
+
+        def words_of(g):
+            return x_words[g].rearrange("p c r -> p (c r)").bitcast(I32)
+
+        w_rows = w1.rearrange("(g p j) n -> g p j n", g=2, j=PACK)
+        cache_rows = cache.rearrange("(p t) c -> t p c", t=PACK)
+        out_rows = out_0.rearrange("(p t) c -> t p c", t=PACK)
+
+        def load_w(g, h):
+            nc.sync.dma_start(w_raw[g][h][:], w_rows[g][:, :, h * 256 : (h + 1) * 256])
+
+        nc.sync.dma_start(offs_sb[:], offs)
+        load_w(0, 0)
+        for q in range(4):
+            nc.sync.dma_start(xs[32 * q : 32 * q + 8, :].bitcast(I32), x_scales[:, 4 * q : 4 * q + 4, :].bitcast(I32))
+        nc.sync.dma_start(scale_rows[:], scale[0:32, :].rearrange("a (b p) -> (a b) p", p=P))
+        nc.scalar.activation(warm[:, 1:2], warm[:, 0:1], TANH)
+        nc.sync.dma_start(xw[0][:].bitcast(I32), words_of(0))
+        load_w(0, 1)
+        load_w(1, 0)
+        load_w(1, 1)
+        nc.sync.dma_start(xw[1][:].bitcast(I32), words_of(1))
+        nc.sync.dma_start(scale_sb[:], scale)
+        nc.sync.dma_start(slot_sb[:], slot)
+        for t in range(PACK):
+            nc.sync.dma_start(window[t][:], cache_rows[t])
+
+        xg0 = sb("xg0", [P, S], U32)
+        xg1 = [sb("xg1_%d" % b, [P, P], U32) for b in range(BLOCKS)]
+        sg = sb("sg", [P, S], U8)
+        grouped = [sb("grouped%d" % g, [P, PACK * N], BF16) for g in range(2)]
+        wq = [sb("wq%d" % g, [P, N], U32) for g in range(2)]
+        ws = [sb("ws%d" % g, [P, N], U8) for g in range(2)]
+
+        def deal(g, h):
+            src = w_raw[g][h][:].rearrange("p j (m t) -> p m j t", t=PACK)
+            dst = grouped[g][:].rearrange("p (t m j) -> p m j t", t=PACK, j=PACK)[:, 64 * h : 64 * (h + 1)]
+            cut = 64 - ON_SCALAR[2 * g + h]
+            if cut > 0:
+                nc.vector.tensor_copy(dst[:, 0:cut], src[:, 0:cut])
+            nc.scalar.copy(dst[:, cut:64], src[:, cut:64])
+
+        def quantise_w(g, first, last):
+            nc.vector.quantize_mx(
+                out=wq[g][:, first * P : last * P].bitcast(FP8X4),
+                scales=ws[g][:, first * P : last * P],
+                in_=grouped[g][:, first * PACK * P : last * PACK * P],
+            )
+
+        def tokens(g, b):
+            words = xg0[:, b * P : (b + 1) * P] if g == 0 else xg1[b][:]
+            return words.bitcast(FP8X4), sg[4 * g : P, b * P : (b + 1) * P]
+
+        def weights(g, first, last):
+            return wq[g][:, first * P : last * P].bitcast(FP8X4), ws[g][:, first * P : last * P]
+
+        def product(out, still, moving, g):
+            nc.tensor.matmul_mx(out=out, lhsT=still[0], lhsT_scale=still[1], rhs=moving[0], rhs_scale=moving[1], start=(g == 0), stop=(g == 1))
+
+        deal(0, 0)
+        nc.vector.tensor_copy(sg[:], xs[:].indirect(offs_sb[:]))
+        nc.vector.tensor_copy(xg0[:], xw[0][:].indirect(offs_sb[:]))
+
+        scale_ps = bank("scale_ps", 7)
+        nc.tensor.transpose(scale_ps[:, 0:P], scale_rows[:], ident[:])
+        factor = sb("factor", [P, BLOCKS], F32)
+        nc.scalar.copy(factor[:], scale_ps[:, 0:BLOCKS])
+
+        deal(0, 1)
+        quantise_w(0, 0, 4)
+        direct = [bank("direct%d" % b, b) for b in range(BLOCKS)]
+        y = [bank("y%d" % b, 4 + b) for b in range(BLOCKS)]
+        for b in range(BLOCKS):
+            product(direct[b][:, 0:P], weights(0, 0, 1), tokens(0, b), 0)
+        for b in range(BLOCKS):
+            product(y[b][:, 0:256], tokens(0, b), weights(0, 1, 3), 0)
+        deal(1, 0)
+        deal(1, 1)
+        quantise_w(1, 0, 1)
+        per = P // LIST_ROWS
+        nc.vector.tensor_copy(xg1[0][:], xw[1][:].indirect(offs_sb[:, 0:per]))
+        quantise_w(1, 1, 3)
+        for b in range(1, BLOCKS):
+            nc.vector.tensor_copy(xg1[b][:], xw[1][:].indirect(offs_sb[:, b * per : (b + 1) * per]))
+        quantise_w(1, 3, 4)
+
+        scaled = sb("scaled", [P, S], F32, "first")
+        r0 = [sb("r0_%d" % h, [P, 2 * P], F32) for h in range(2)]
+        r = [None] + [sb("r%d" % t, [P, S], F32) for t in range(1, PACK)]
+
+        for b in range(BLOCKS):
+            product(direct[b][:, 0:P], weights(1, 0, 1), tokens(1, b), 1)
+            nc.vector.tensor_tensor(scaled[:, b * P : (b + 1) * P], direct[b][:, 0:P], scale_sb[:, b * P : (b + 1) * P], MULT)
+            nc.scalar.activation(r0[b // 2][:, (b % 2) * P : (b % 2 + 1) * P], scaled[:, b * P : (b + 1) * P], TANH)
+        z12 = sb("z12", [P, BLOCKS * 2 * P], F32, "first")
+        for b in range(BLOCKS):
+            product(y[b][:, 0:256], tokens(1, b), weights(1, 1, 3), 1)
+            nc.scalar.activation(z12[:, 2 * b * P : 2 * (b + 1) * P], y[b][:, 0:256], TANH, scale=factor[:, b : b + 1])
+        for h in range(2):
+            nc.vector.tensor_copy(window[0][:].indirect(slot_sb[:, 2 * h * per : 2 * (h + 1) * per]), r0[h][:])
+        nc.sync.dma_start(out_rows[0], window[0][:])
+
+        def turn_and_scatter(t, pieces):
+            turned = bank("turned%d" % t, (0, 1, 3)[t - 1])
+            for b in range(BLOCKS):
+                nc.tensor.transpose(turned[:, b * P : (b + 1) * P], pieces[b], ident[:])
+            nc.scalar.copy(r[t][:], turned[:])
+            nc.vector.tensor_copy(window[t][:].indirect(slot_sb[:]), r[t][:])
+            nc.sync.dma_start(out_rows[t], window[t][:])
+        y3 = bank("y3last", 2)
+        for b in range(BLOCKS):
+            for g in range(2):
+                product(y3[:, b * P : (b + 1) * P], tokens(g, b), weights(g, 3, 4), g)
+        z3 = [sb("z3_%d" % b, [P, P], F32, "woven%d" % (3 - b) if b > 0 else None) for b in range(BLOCKS)]
+        for b in range(BLOCKS):
+            nc.scalar.activation(z3[b][:], y3[:, b * P : (b + 1) * P], TANH, scale=factor[:, b : b + 1])
+        turn_and_scatter(1, [z12[:, 2 * b * P : (2 * b + 1) * P] for b in range(BLOCKS)])
+        turn_and_scatter(2, [z12[:, (2 * b + 1) * P : (2 * b + 2) * P] for b in range(BLOCKS)])
+        turn_and_scatter(3, [z3[b][:] for b in range(BLOCKS)])
+
+        Q = U // 4
+        spans = ((0, 2 * Q), (2 * Q, 3 * Q), (3 * Q, 4 * Q))
+        woven = [sb("woven%d" % c, [P, hi - lo, PACK], BF16) for c, (lo, hi) in enumerate(spans)]
+        codes = sb("codes", [P, U], U32)
+        plane = sb("plane", [P, U], U8)
+        on_vector = 2
+        for t in range(2):
+            for c, (lo, hi) in enumerate(spans):
+                nc.scalar.copy(woven[c][:, :, t], window[t][:, lo:hi])
+        for c, (lo, hi) in enumerate(spans):
+            cols = window[2][:, lo:hi]
+            if c < on_vector:
+                nc.scalar.copy(woven[c][:, :, 2:4], cols.unsqueeze(2).to_broadcast([P, hi - lo, 2]))
+            else:
+                nc.scalar.copy(woven[c][:, :, 2], cols)
+        for c, (lo, hi) in enumerate(spans):
+            if c < on_vector:
+                nc.vector.tensor_copy(woven[c][:, :, 3], window[3][:, lo:hi])
+            else:
+                nc.scalar.copy(woven[c][:, :, 3], window[3][:, lo:hi])
+        out_words = out_1[0].rearrange("p c r -> p (c r)").bitcast(I32)
+        for c, (lo, hi) in enumerate(spans):
+            nc.vector.quantize_mx(out=codes[:, lo:hi].bitcast(FP8X4), scales=plane[:, lo:hi], in_=woven[c][:].rearrange("p c t -> p (c t)"))
+            nc.sync.dma_start(out_words[:, lo:hi], codes[:, lo:hi].bitcast(I32))
+        for q in range(4):
+            queue = nc.sync if q % 2 == 0 else nc.scalar
+            queue.dma_start(out_2[0, 4 * q : 4 * q + 4, :].bitcast(I32), plane[32 * q : 32 * q + 4, :].bitcast(I32))

@@ -20,7 +20,7 @@ P = 128
 PACK = 4
 LIST_ROWS = 16
 BLOCKS = S // P
-ON_SCALAR = (64, 24, 32, 20)
+ON_SCALAR = (64, 32)
 
 
 def tile_picked_zkvw_tanh_po_kernel(tc, x_words, x_scales, cache, w1, scale, offs, slot, out_0, out_1, out_2):
@@ -64,32 +64,44 @@ def tile_picked_zkvw_tanh_po_kernel(tc, x_words, x_scales, cache, w1, scale, off
         load_w(0, 0)
         for q in range(4):
             nc.sync.dma_start(xs[32 * q : 32 * q + 8, :].bitcast(I32), x_scales[:, 4 * q : 4 * q + 4, :].bitcast(I32))
-        nc.sync.dma_start(scale_rows[:], scale[0:32, :].rearrange("a (b p) -> (a b) p", p=P))
         nc.scalar.activation(warm[:, 1:2], warm[:, 0:1], TANH)
         nc.sync.dma_start(xw[0][:].bitcast(I32), words_of(0))
         load_w(0, 1)
+        nc.sync.dma_start(xw[1][:].bitcast(I32), words_of(1))
         load_w(1, 0)
         load_w(1, 1)
-        nc.sync.dma_start(xw[1][:].bitcast(I32), words_of(1))
+        nc.sync.dma_start(scale_rows[:], scale[0:32, :].rearrange("a (b p) -> (a b) p", p=P))
         nc.sync.dma_start(scale_sb[:], scale)
         nc.sync.dma_start(slot_sb[:], slot)
         for t in range(PACK):
             nc.sync.dma_start(window[t][:], cache_rows[t])
 
-        xg0 = sb("xg0", [P, S], U32)
-        xg1 = [sb("xg1_%d" % b, [P, P], U32) for b in range(BLOCKS)]
+        xg = [sb("xg%d" % g, [P, S], U32) for g in range(2)]
         sg = sb("sg", [P, S], U8)
         grouped = [sb("grouped%d" % g, [P, PACK * N], BF16) for g in range(2)]
         wq = [sb("wq%d" % g, [P, N], U32) for g in range(2)]
         ws = [sb("ws%d" % g, [P, N], U8) for g in range(2)]
 
-        def deal(g, h):
+        def views(g, h):
             src = w_raw[g][h][:].rearrange("p j (m t) -> p m j t", t=PACK)
             dst = grouped[g][:].rearrange("p (t m j) -> p m j t", t=PACK, j=PACK)[:, 64 * h : 64 * (h + 1)]
-            cut = 64 - ON_SCALAR[2 * g + h]
+            return dst, src
+
+        def deal_first(h):
+            dst, src = views(0, h)
+            cut = 64 - ON_SCALAR[h]
             if cut > 0:
                 nc.vector.tensor_copy(dst[:, 0:cut], src[:, 0:cut])
             nc.scalar.copy(dst[:, cut:64], src[:, cut:64])
+
+        def deal_second(h):
+            dst, src = views(1, h)
+            if h == 0:
+                nc.vector.tensor_copy(dst[:, :, :, 0:2], src[:, :, :, 0:2])
+            else:
+                nc.vector.tensor_copy(dst[:, :, :, 0], src[:, :, :, 0])
+                nc.vector.tensor_copy(dst[:, :, :, 1], src[:, :, :, 1])
+            nc.scalar.copy(dst[:, :, :, 2:4], src[:, :, :, 2:4])
 
         def quantise_w(g, first, last):
             nc.vector.quantize_mx(
@@ -98,9 +110,8 @@ def tile_picked_zkvw_tanh_po_kernel(tc, x_words, x_scales, cache, w1, scale, off
                 in_=grouped[g][:, first * PACK * P : last * PACK * P],
             )
 
-        def tokens(g, b):
-            words = xg0[:, b * P : (b + 1) * P] if g == 0 else xg1[b][:]
-            return words.bitcast(FP8X4), sg[4 * g : P, b * P : (b + 1) * P]
+        def tokens(g, lo, hi):
+            return xg[g][:, lo * P : hi * P].bitcast(FP8X4), sg[4 * g : P, lo * P : hi * P]
 
         def weights(g, first, last):
             return wq[g][:, first * P : last * P].bitcast(FP8X4), ws[g][:, first * P : last * P]
@@ -108,69 +119,73 @@ def tile_picked_zkvw_tanh_po_kernel(tc, x_words, x_scales, cache, w1, scale, off
         def product(out, still, moving, g):
             nc.tensor.matmul_mx(out=out, lhsT=still[0], lhsT_scale=still[1], rhs=moving[0], rhs_scale=moving[1], start=(g == 0), stop=(g == 1))
 
-        deal(0, 0)
+        deal_first(0)
         nc.vector.tensor_copy(sg[:], xs[:].indirect(offs_sb[:]))
-        nc.vector.tensor_copy(xg0[:], xw[0][:].indirect(offs_sb[:]))
+        nc.vector.tensor_copy(xg[0][:], xw[0][:].indirect(offs_sb[:]))
 
-        scale_ps = bank("scale_ps", 7)
+        deal_first(1)
+        nc.vector.tensor_copy(xg[1][:], xw[1][:].indirect(offs_sb[:]))
+        quantise_w(0, 0, 4)
+        runs = ((0, 1), (1, 2), (2, 4))
+        direct = [bank("direct%d" % i, i) for i in range(len(runs))]
+        y = [bank("y%d" % b, 4 + b) for b in range(BLOCKS)]
+        for i, (lo, hi) in enumerate(runs):
+            product(direct[i][:, 0 : (hi - lo) * P], weights(0, 0, 1), tokens(0, lo, hi), 0)
+        for b in range(BLOCKS):
+            product(y[b][:, 0:256], tokens(0, b, b + 1), weights(0, 1, 3), 0)
+        deal_second(0)
+        deal_second(1)
+        scale_ps = bank("scale_ps", 3)
         nc.tensor.transpose(scale_ps[:, 0:P], scale_rows[:], ident[:])
         factor = sb("factor", [P, BLOCKS], F32)
         nc.scalar.copy(factor[:], scale_ps[:, 0:BLOCKS])
 
-        deal(0, 1)
-        quantise_w(0, 0, 4)
-        direct = [bank("direct%d" % b, b) for b in range(BLOCKS)]
-        y = [bank("y%d" % b, 4 + b) for b in range(BLOCKS)]
-        for b in range(BLOCKS):
-            product(direct[b][:, 0:P], weights(0, 0, 1), tokens(0, b), 0)
-        for b in range(BLOCKS):
-            product(y[b][:, 0:256], tokens(0, b), weights(0, 1, 3), 0)
-        deal(1, 0)
-        deal(1, 1)
         quantise_w(1, 0, 1)
-        per = P // LIST_ROWS
-        nc.vector.tensor_copy(xg1[0][:], xw[1][:].indirect(offs_sb[:, 0:per]))
         quantise_w(1, 1, 3)
-        for b in range(1, BLOCKS):
-            nc.vector.tensor_copy(xg1[b][:], xw[1][:].indirect(offs_sb[:, b * per : (b + 1) * per]))
         quantise_w(1, 3, 4)
+        per = P // LIST_ROWS
 
-        scaled = sb("scaled", [P, S], F32, "first")
-        r0 = [sb("r0_%d" % h, [P, 2 * P], F32) for h in range(2)]
+        scaled = [sb("scaled%d" % i, [P, (hi - lo) * P], F32, "woven%d" % (i + 1)) for i, (lo, hi) in enumerate(runs)]
+        r0_head = sb("r0_head", [P, P], F32)
+        r0_rest = sb("r0_rest", [P, S - P], F32)
         r = [None] + [sb("r%d" % t, [P, S], F32) for t in range(1, PACK)]
 
+        for i, (lo, hi) in enumerate(runs):
+            cols = slice(lo * P, hi * P)
+            product(direct[i][:, 0 : (hi - lo) * P], weights(1, 0, 1), tokens(1, lo, hi), 1)
+            nc.vector.tensor_tensor(scaled[i][:], direct[i][:, 0 : (hi - lo) * P], scale_sb[:, cols], MULT)
+            bounded = r0_head[:] if i == 0 else r0_rest[:, (lo - 1) * P : (hi - 1) * P]
+            nc.scalar.activation(bounded, scaled[i][:], TANH)
+        z1 = [sb("z1_%d" % b, [P, P], F32, "woven%d" % (3 - b)) for b in range(BLOCKS)]
         for b in range(BLOCKS):
-            product(direct[b][:, 0:P], weights(1, 0, 1), tokens(1, b), 1)
-            nc.vector.tensor_tensor(scaled[:, b * P : (b + 1) * P], direct[b][:, 0:P], scale_sb[:, b * P : (b + 1) * P], MULT)
-            nc.scalar.activation(r0[b // 2][:, (b % 2) * P : (b % 2 + 1) * P], scaled[:, b * P : (b + 1) * P], TANH)
-        z12 = sb("z12", [P, BLOCKS * 2 * P], F32, "first")
-        for b in range(BLOCKS):
-            product(y[b][:, 0:256], tokens(1, b), weights(1, 1, 3), 1)
-            nc.scalar.activation(z12[:, 2 * b * P : 2 * (b + 1) * P], y[b][:, 0:256], TANH, scale=factor[:, b : b + 1])
-        for h in range(2):
-            nc.vector.tensor_copy(window[0][:].indirect(slot_sb[:, 2 * h * per : 2 * (h + 1) * per]), r0[h][:])
+            product(y[b][:, 0:256], tokens(1, b, b + 1), weights(1, 1, 3), 1)
+            nc.scalar.activation(z1[b][:], y[b][:, 0:P], TANH, scale=factor[:, b : b + 1])
+        nc.vector.tensor_copy(window[0][:].indirect(slot_sb[:, 0:per]), r0_head[:])
+        nc.vector.tensor_copy(window[0][:].indirect(slot_sb[:, per : BLOCKS * per]), r0_rest[:])
         nc.sync.dma_start(out_rows[0], window[0][:])
 
         def turn_and_scatter(t, pieces):
-            turned = bank("turned%d" % t, (0, 1, 3)[t - 1])
+            turned = bank("turned%d" % t, t - 1)
             for b in range(BLOCKS):
                 nc.tensor.transpose(turned[:, b * P : (b + 1) * P], pieces[b], ident[:])
             nc.scalar.copy(r[t][:], turned[:])
             nc.vector.tensor_copy(window[t][:].indirect(slot_sb[:]), r[t][:])
             nc.sync.dma_start(out_rows[t], window[t][:])
-        y3 = bank("y3last", 2)
+
+        turn_and_scatter(1, [z1[b][:] for b in range(BLOCKS)])
+        z23 = [sb("z23_%d" % b, [P, 2 * P], F32, "woven%d" % (3 - b)) for b in range(BLOCKS)]
+        for b in range(BLOCKS):
+            nc.scalar.activation(z23[b][:, 0:P], y[b][:, P : 2 * P], TANH, scale=factor[:, b : b + 1])
+        y3 = bank("y3last", 3)
         for b in range(BLOCKS):
             for g in range(2):
-                product(y3[:, b * P : (b + 1) * P], tokens(g, b), weights(g, 3, 4), g)
-        z3 = [sb("z3_%d" % b, [P, P], F32, "woven%d" % (3 - b) if b > 0 else None) for b in range(BLOCKS)]
+                product(y3[:, b * P : (b + 1) * P], tokens(g, b, b + 1), weights(g, 3, 4), g)
         for b in range(BLOCKS):
-            nc.scalar.activation(z3[b][:], y3[:, b * P : (b + 1) * P], TANH, scale=factor[:, b : b + 1])
-        turn_and_scatter(1, [z12[:, 2 * b * P : (2 * b + 1) * P] for b in range(BLOCKS)])
-        turn_and_scatter(2, [z12[:, (2 * b + 1) * P : (2 * b + 2) * P] for b in range(BLOCKS)])
-        turn_and_scatter(3, [z3[b][:] for b in range(BLOCKS)])
+            nc.scalar.activation(z23[b][:, P : 2 * P], y3[:, b * P : (b + 1) * P], TANH, scale=factor[:, b : b + 1])
+        turn_and_scatter(2, [z23[b][:, 0:P] for b in range(BLOCKS)])
+        turn_and_scatter(3, [z23[b][:, P : 2 * P] for b in range(BLOCKS)])
 
-        Q = U // 4
-        spans = ((0, 2 * Q), (2 * Q, 3 * Q), (3 * Q, 4 * Q))
+        spans = ((0, 512), (512, 768), (768, 1024))
         woven = [sb("woven%d" % c, [P, hi - lo, PACK], BF16) for c, (lo, hi) in enumerate(spans)]
         codes = sb("codes", [P, U], U32)
         plane = sb("plane", [P, U], U8)

@@ -192,7 +192,11 @@ def tile_picked_zkvw_tanh_po_kernel(tc, x_words, x_scales, cache, w1, scale, off
         on_vector = 2
         for t in range(2):
             for c, (lo, hi) in enumerate(spans):
-                nc.scalar.copy(woven[c][:, :, t], window[t][:, lo:hi])
+                if (t, c) == (0, 0):
+                    both = window[0][:, lo:hi].unsqueeze(2).to_broadcast([P, hi - lo, 2])
+                    nc.gpsimd.tensor_scalar(woven[0][:, :, 0:2], both, 1.0, 0.0, MULT, mybir.AluOpType.add)
+                else:
+                    nc.scalar.copy(woven[c][:, :, t], window[t][:, lo:hi])
         for c, (lo, hi) in enumerate(spans):
             cols = window[2][:, lo:hi]
             if c < on_vector:

@@ -44,11 +44,9 @@ def tile_picked_zkvw_tanh_po_kernel(tc, x_words, x_scales, cache, w1, scale, off
         scale_sb = sb("scale_sb", [P, S], F32)
         window = [sb("window%d" % t, [P, U], F32) for t in range(PACK)]
         ident = sb("ident", [P, P], F32)
-        warm = sb("warm", [P, 2], F32)
 
         nc.gpsimd.memset(xs[:].bitcast(I32), 0)
         make_identity(nc, ident[:])
-        nc.vector.memset(warm[:, 0:1], 0.0)
 
         def words_of(g):
             return x_words[g].rearrange("p c r -> p (c r)").bitcast(I32)
@@ -64,7 +62,6 @@ def tile_picked_zkvw_tanh_po_kernel(tc, x_words, x_scales, cache, w1, scale, off
         load_w(0, 0)
         for q in range(4):
             nc.sync.dma_start(xs[32 * q : 32 * q + 8, :].bitcast(I32), x_scales[:, 4 * q : 4 * q + 4, :].bitcast(I32))
-        nc.scalar.activation(warm[:, 1:2], warm[:, 0:1], TANH)
         nc.sync.dma_start(xw[0][:].bitcast(I32), words_of(0))
         load_w(0, 1)
         nc.sync.dma_start(xw[1][:].bitcast(I32), words_of(1))

@@ -142,7 +142,7 @@ def tile_picked_zkvw_tanh_po_kernel(tc, x_words, x_scales, cache, w1, scale, off
         quantise_w(1, 3, 4)
         per = P // LIST_ROWS
 
-        scaled = [sb("scaled%d" % i, [P, (hi - lo) * P], F32, "woven%d" % (i + 1)) for i, (lo, hi) in enumerate(runs)]
+        scaled = [sb("scaled%d" % i, [P, (hi - lo) * P], F32, "stage%d" % (i + 1)) for i, (lo, hi) in enumerate(runs)]
         r0_head = sb("r0_head", [P, P], F32)
         r0_rest = sb("r0_rest", [P, S - P], F32)
         r = [None] + [sb("r%d" % t, [P, S], F32) for t in range(1, PACK)]
@@ -153,7 +153,7 @@ def tile_picked_zkvw_tanh_po_kernel(tc, x_words, x_scales, cache, w1, scale, off
             nc.vector.tensor_tensor(scaled[i][:], direct[i][:, 0 : (hi - lo) * P], scale_sb[:, cols], MULT)
             bounded = r0_head[:] if i == 0 else r0_rest[:, (lo - 1) * P : (hi - 1) * P]
             nc.scalar.activation(bounded, scaled[i][:], TANH)
-        z1 = [sb("z1_%d" % b, [P, P], F32, "woven%d" % (3 - b)) for b in range(BLOCKS)]
+        z1 = [sb("z1_%d" % b, [P, P], F32, "stage%d" % (3 - b)) for b in range(BLOCKS)]
         for b in range(BLOCKS):
             product(y[b][:, 0:256], tokens(1, b, b + 1), weights(1, 1, 3), 1)
             nc.scalar.activation(z1[b][:], y[b][:, 0:P], TANH, scale=factor[:, b : b + 1])
@@ -170,7 +170,7 @@ def tile_picked_zkvw_tanh_po_kernel(tc, x_words, x_scales, cache, w1, scale, off
             nc.sync.dma_start(out_rows[t], window[t][:])
 
         turn_and_scatter(1, [z1[b][:] for b in range(BLOCKS)])
-        z23 = [sb("z23_%d" % b, [P, 2 * P], F32, "woven%d" % (3 - b)) for b in range(BLOCKS)]
+        z23 = [sb("z23_%d" % b, [P, 2 * P], F32, "stage%d" % (3 - b)) for b in range(BLOCKS)]
         for b in range(BLOCKS):
             nc.scalar.activation(z23[b][:, 0:P], y[b][:, P : 2 * P], TANH, scale=factor[:, b : b + 1])
         y3 = bank("y3last", 3)
@@ -187,19 +187,23 @@ def tile_picked_zkvw_tanh_po_kernel(tc, x_words, x_scales, cache, w1, scale, off
         codes = sb("codes", [P, U], U32)
         plane = sb("plane", [P, U], U8)
         on_vector = 2
-        for t in range(2):
-            for c, (lo, hi) in enumerate(spans):
-                if (t, c) == (0, 0):
-                    both = window[0][:, lo:hi].unsqueeze(2).to_broadcast([P, hi - lo, 2])
-                    nc.gpsimd.tensor_scalar(woven[0][:, :, 0:2], both, 1.0, 0.0, MULT, mybir.AluOpType.add)
-                else:
-                    nc.scalar.copy(woven[c][:, :, t], window[t][:, lo:hi])
-        for c, (lo, hi) in enumerate(spans):
-            cols = window[2][:, lo:hi]
-            if c < on_vector:
-                nc.scalar.copy(woven[c][:, :, 2:4], cols.unsqueeze(2).to_broadcast([P, hi - lo, 2]))
-            else:
-                nc.scalar.copy(woven[c][:, :, 2], cols)
+
+        def spread(t, c, last):
+            lo, hi = spans[c]
+            return woven[c][:, :, t:last], window[t][:, lo:hi].unsqueeze(2).to_broadcast([P, hi - lo, last - t])
+
+        def weave_on_gpsimd(t, c, last):
+            dst, src = spread(t, c, last)
+            nc.gpsimd.tensor_scalar(dst, src, 1.0, -0.0, MULT, mybir.AluOpType.add)
+
+        for c in range(len(spans)):
+            weave_on_gpsimd(0, c, 1)
+        for c in range(len(spans)):
+            weave_on_gpsimd(1, c, PACK)
+        for c in range(on_vector):
+            dst, src = spread(2, c, PACK)
+            nc.scalar.copy(dst, src)
+        weave_on_gpsimd(2, on_vector, PACK)
         for c, (lo, hi) in enumerate(spans):
             if c < on_vector:
                 nc.vector.tensor_copy(woven[c][:, :, 3], window[3][:, lo:hi])

@@ -58,8 +58,8 @@ def tile_picked_zkvw_tanh_po_kernel(tc, x_words, x_scales, cache, w1, scale, off
         def load_w(g, h):
             nc.sync.dma_start(w_raw[g][h][:], w_rows[g][:, :, h * 256 : (h + 1) * 256])
 
-        nc.sync.dma_start(offs_sb[:], offs)
         load_w(0, 0)
+        nc.sync.dma_start(offs_sb[:], offs)
         for q in range(4):
             nc.sync.dma_start(xs[32 * q : 32 * q + 8, :].bitcast(I32), x_scales[:, 4 * q : 4 * q + 4, :].bitcast(I32))
         nc.sync.dma_start(xw[0][:].bitcast(I32), words_of(0))
@@ -67,10 +67,11 @@ def tile_picked_zkvw_tanh_po_kernel(tc, x_words, x_scales, cache, w1, scale, off
         nc.sync.dma_start(xw[1][:].bitcast(I32), words_of(1))
         load_w(1, 0)
         load_w(1, 1)
-        nc.sync.dma_start(scale_rows[:], scale[0:32, :].rearrange("a (b p) -> (a b) p", p=P))
         nc.sync.dma_start(scale_sb[:], scale)
         nc.sync.dma_start(slot_sb[:], slot)
-        for t in range(PACK):
+        nc.sync.dma_start(window[0][:], cache_rows[0])
+        nc.sync.dma_start(scale_rows[:], scale[0:32, :].rearrange("a (b p) -> (a b) p", p=P))
+        for t in range(1, PACK):
             nc.sync.dma_start(window[t][:], cache_rows[t])
 
         xg = [sb("xg%d" % g, [P, S], U32) for g in range(2)]
@@ -205,7 +206,10 @@ def tile_picked_zkvw_tanh_po_kernel(tc, x_words, x_scales, cache, w1, scale, off
             nc.scalar.copy(dst, src)
         weave_on_gpsimd(2, on_vector, PACK)
         for c, (lo, hi) in enumerate(spans):
-            if c < on_vector:
+            if c == 0:
+                nc.vector.tensor_copy(woven[c][:, 0:320, 3], window[3][:, 0:320])
+                nc.scalar.copy(woven[c][:, 320:hi, 3], window[3][:, 320:hi])
+            elif c == 1:
                 nc.vector.tensor_copy(woven[c][:, :, 3], window[3][:, lo:hi])
             else:
                 nc.scalar.copy(woven[c][:, :, 3], window[3][:, lo:hi])
@@ -214,5 +218,5 @@ def tile_picked_zkvw_tanh_po_kernel(tc, x_words, x_scales, cache, w1, scale, off
             nc.vector.quantize_mx(out=codes[:, lo:hi].bitcast(FP8X4), scales=plane[:, lo:hi], in_=woven[c][:].rearrange("p c t -> p (c t)"))
             nc.sync.dma_start(out_words[:, lo:hi], codes[:, lo:hi].bitcast(I32))
         for q in range(4):
-            queue = nc.sync if q % 2 == 0 else nc.scalar
+            queue = nc.sync if q == 0 else nc.scalar
             queue.dma_start(out_2[0, 4 * q : 4 * q + 4, :].bitcast(I32), plane[32 * q : 32 * q + 4, :].bitcast(I32))

@@ -15,12 +15,13 @@ U8 = mybir.dt.uint8
 FP8X4 = mybir.dt.float8_e4m3fn_x4
 TANH = mybir.ActivationFunctionType.Tanh
 MULT = mybir.AluOpType.mult
+ADD = mybir.AluOpType.add
 
 P = 128
 PACK = 4
 LIST_ROWS = 16
 BLOCKS = S // P
-ON_SCALAR = (64, 32)
+HALF = N // 2
 
 
 def tile_picked_zkvw_tanh_po_kernel(tc, x_words, x_scales, cache, w1, scale, offs, slot, out_0, out_1, out_2):
@@ -39,9 +40,8 @@ def tile_picked_zkvw_tanh_po_kernel(tc, x_words, x_scales, cache, w1, scale, off
         slot_sb = sb("slot_sb", [P, S // LIST_ROWS], U16)
         xw = [sb("xw%d" % g, [P, T], U32) for g in range(2)]
         xs = sb("xs", [P, T], U8)
-        w_raw = [[sb("w_raw%d_%d" % (g, h), [P, PACK, N // 2], F32) for h in range(2)] for g in range(2)]
+        w_raw = [[sb("w_raw%d_%d" % (g, h), [P, PACK, HALF], F32) for h in range(2)] for g in range(2)]
         scale_rows = sb("scale_rows", [P, P], F32)
-        scale_sb = sb("scale_sb", [P, S], F32)
         window = [sb("window%d" % t, [P, U], F32) for t in range(PACK)]
         ident = sb("ident", [P, P], F32)
 
@@ -52,164 +52,166 @@ def tile_picked_zkvw_tanh_po_kernel(tc, x_words, x_scales, cache, w1, scale, off
             return x_words[g].rearrange("p c r -> p (c r)").bitcast(I32)
 
         w_rows = w1.rearrange("(g p j) n -> g p j n", g=2, j=PACK)
-        cache_rows = cache.rearrange("(p t) c -> t p c", t=PACK)
-        out_rows = out_0.rearrange("(p t) c -> t p c", t=PACK)
+
+        def rows_of(matrix, t):
+            by_word = matrix.rearrange("(l r) c -> l r c", r=PACK)
+            if t < 2:
+                return by_word[64 * t : 64 * (t + 1), 0:2, :]
+            return by_word[:, t, :]
 
         def load_w(g, h):
-            nc.sync.dma_start(w_raw[g][h][:], w_rows[g][:, :, h * 256 : (h + 1) * 256])
+            nc.sync.dma_start(w_raw[g][h][:], w_rows[g][:, :, h * HALF : (h + 1) * HALF])
 
-        load_w(0, 0)
         nc.sync.dma_start(offs_sb[:], offs)
         for q in range(4):
             nc.sync.dma_start(xs[32 * q : 32 * q + 8, :].bitcast(I32), x_scales[:, 4 * q : 4 * q + 4, :].bitcast(I32))
         nc.sync.dma_start(xw[0][:].bitcast(I32), words_of(0))
-        load_w(0, 1)
-        nc.sync.dma_start(xw[1][:].bitcast(I32), words_of(1))
-        load_w(1, 0)
-        load_w(1, 1)
-        nc.sync.dma_start(scale_sb[:], scale)
-        nc.sync.dma_start(slot_sb[:], slot)
-        nc.sync.dma_start(window[0][:], cache_rows[0])
         nc.sync.dma_start(scale_rows[:], scale[0:32, :].rearrange("a (b p) -> (a b) p", p=P))
-        for t in range(1, PACK):
-            nc.sync.dma_start(window[t][:], cache_rows[t])
+        nc.sync.dma_start(xw[1][:].bitcast(I32), words_of(1))
+        load_w(0, 0)
+        load_w(1, 0)
+        load_w(0, 1)
+        nc.sync.dma_start(slot_sb[:], slot)
+        load_w(1, 1)
+        for t in range(PACK):
+            nc.sync.dma_start(window[t][:], rows_of(cache, t))
 
         xg = [sb("xg%d" % g, [P, S], U32) for g in range(2)]
         sg = sb("sg", [P, S], U8)
-        grouped = [sb("grouped%d" % g, [P, PACK * N], BF16) for g in range(2)]
-        wq = [sb("wq%d" % g, [P, N], U32) for g in range(2)]
-        ws = [sb("ws%d" % g, [P, N], U8) for g in range(2)]
+        grouped = [[[sb("grouped%d_%d_%d" % (g, h, u), [P, PACK * P], BF16) for u in range(2)] for h in range(2)] for g in range(2)]
+        low_q = [[sb("low_q%d_%d" % (g, h), [P, P], U32) for h in range(2)] for g in range(2)]
+        low_s = [[sb("low_s%d_%d" % (g, h), [P, P], U8) for h in range(2)] for g in range(2)]
+        high_q = [sb("high_q%d" % g, [P, 2 * P], U32) for g in range(2)]
+        high_s = [sb("high_s%d" % g, [P, 2 * P], U8) for g in range(2)]
 
-        def views(g, h):
-            src = w_raw[g][h][:].rearrange("p j (m t) -> p m j t", t=PACK)
-            dst = grouped[g][:].rearrange("p (t m j) -> p m j t", t=PACK, j=PACK)[:, 64 * h : 64 * (h + 1)]
-            return dst, src
-
-        def deal_first(h):
-            dst, src = views(0, h)
-            cut = 64 - ON_SCALAR[h]
-            if cut > 0:
-                nc.vector.tensor_copy(dst[:, 0:cut], src[:, 0:cut])
-            nc.scalar.copy(dst[:, cut:64], src[:, cut:64])
-
-        def deal_second(h):
-            dst, src = views(1, h)
-            if h == 0:
-                nc.vector.tensor_copy(dst[:, :, :, 0:2], src[:, :, :, 0:2])
+        def deal(g, h, u, engine="scalar"):
+            src = w_raw[g][h][:].rearrange("p j (l u e) -> p u l j e", u=2, e=2)[:, u]
+            dst = grouped[g][h][u][:].rearrange("p (l e j) -> p l j e", e=2, j=PACK)
+            if engine == "vector":
+                nc.vector.tensor_copy(dst, src)
             else:
-                nc.vector.tensor_copy(dst[:, :, :, 0], src[:, :, :, 0])
-                nc.vector.tensor_copy(dst[:, :, :, 1], src[:, :, :, 1])
-            nc.scalar.copy(dst[:, :, :, 2:4], src[:, :, :, 2:4])
+                nc.scalar.copy(dst, src)
 
-        def quantise_w(g, first, last):
-            nc.vector.quantize_mx(
-                out=wq[g][:, first * P : last * P].bitcast(FP8X4),
-                scales=ws[g][:, first * P : last * P],
-                in_=grouped[g][:, first * PACK * P : last * PACK * P],
-            )
+        def low(g, h):
+            return low_q[g][h][:].bitcast(FP8X4), low_s[g][h][:]
+
+        def high(g, first, last):
+            return high_q[g][:, first * P : last * P].bitcast(FP8X4), high_s[g][:, first * P : last * P]
+
+        def quantise_w(g, h, u):
+            codes, scales = low(g, h) if u == 0 else high(g, h, h + 1)
+            nc.vector.quantize_mx(out=codes, scales=scales, in_=grouped[g][h][u][:])
 
         def tokens(g, lo, hi):
             return xg[g][:, lo * P : hi * P].bitcast(FP8X4), sg[4 * g : P, lo * P : hi * P]
 
-        def weights(g, first, last):
-            return wq[g][:, first * P : last * P].bitcast(FP8X4), ws[g][:, first * P : last * P]
-
         def product(out, still, moving, g):
             nc.tensor.matmul_mx(out=out, lhsT=still[0], lhsT_scale=still[1], rhs=moving[0], rhs_scale=moving[1], start=(g == 0), stop=(g == 1))
 
-        deal_first(0)
-        nc.vector.tensor_copy(sg[:], xs[:].indirect(offs_sb[:]))
-        nc.vector.tensor_copy(xg[0][:], xw[0][:].indirect(offs_sb[:]))
+        per = P // LIST_ROWS
 
-        deal_first(1)
-        nc.vector.tensor_copy(xg[1][:], xw[1][:].indirect(offs_sb[:]))
-        quantise_w(0, 0, 4)
-        runs = ((0, 1), (1, 2), (2, 4))
-        direct = [bank("direct%d" % i, i) for i in range(len(runs))]
-        y = [bank("y%d" % b, 4 + b) for b in range(BLOCKS)]
-        for i, (lo, hi) in enumerate(runs):
-            product(direct[i][:, 0 : (hi - lo) * P], weights(0, 0, 1), tokens(0, lo, hi), 0)
-        for b in range(BLOCKS):
-            product(y[b][:, 0:256], tokens(0, b, b + 1), weights(0, 1, 3), 0)
-        deal_second(0)
-        deal_second(1)
-        scale_ps = bank("scale_ps", 3)
+        def scatter(t, lo, hi, values):
+            nc.vector.tensor_copy(window[t][:].indirect(slot_sb[:, lo * per : hi * per]), values)
+
+        def turn(pieces, banks, name):
+            result = sb(name, [P, S], F32)
+            share = BLOCKS // len(banks)
+            for i, index in enumerate(banks):
+                turned = bank("turned_%s_%d" % (name, i), index)
+                for b in range(share):
+                    nc.tensor.transpose(turned[:, b * P : (b + 1) * P], pieces[i * share + b], ident[:])
+                nc.scalar.copy(result[:, i * share * P : (i + 1) * share * P], turned[:, 0 : share * P])
+            return result
+
+        def low_products(sums, g, h):
+            for b in range(BLOCKS):
+                product(sums[b][:, 0:P], tokens(g, b, b + 1), low(g, h), g)
+
+        def bound_low(sums, h):
+            bounded = [sb("z%d_%d" % (h, b), [P, P], F32) for b in range(BLOCKS)]
+            for b in range(BLOCKS):
+                nc.scalar.activation(bounded[b][:], sums[b][:, 0:P], TANH, scale=factor[:, b : b + 1])
+            return [piece[:] for piece in bounded]
+
+        nc.vector.tensor_copy(sg[:], xs[:].indirect(offs_sb[:]))
+        for g in range(2):
+            nc.vector.tensor_copy(xg[g][:], xw[g][:].indirect(offs_sb[:]))
+        scale_ps = bank("scale_ps", 0)
         nc.tensor.transpose(scale_ps[:, 0:P], scale_rows[:], ident[:])
         factor = sb("factor", [P, BLOCKS], F32)
         nc.scalar.copy(factor[:], scale_ps[:, 0:BLOCKS])
-
+        y0 = [bank("y0_%d" % b, 4 + b) for b in range(BLOCKS)]
+        deal(0, 0, 0)
+        deal(0, 0, 1)
+        quantise_w(0, 0, 0)
+        low_products(y0, 0, 0)
+        deal(1, 0, 0, "vector")
+        deal(1, 0, 1)
+        quantise_w(0, 0, 1)
+        quantise_w(1, 0, 0)
+        low_products(y0, 1, 0)
+        r0 = turn(bound_low(y0, 0), (0, 1), "r0")
+        deal(0, 1, 0, "vector")
+        deal(0, 1, 1, "vector")
         quantise_w(1, 0, 1)
-        quantise_w(1, 1, 3)
-        quantise_w(1, 3, 4)
-        per = P // LIST_ROWS
+        quantise_w(0, 1, 0)
+        quantise_w(0, 1, 1)
+        deal(1, 1, 0, "vector")
+        deal(1, 1, 1, "vector")
+        quantise_w(1, 1, 0)
+        quantise_w(1, 1, 1)
+        scatter(0, 0, BLOCKS, r0[:])
 
-        scaled = [sb("scaled%d" % i, [P, (hi - lo) * P], F32, "stage%d" % (i + 1)) for i, (lo, hi) in enumerate(runs)]
-        r0_head = sb("r0_head", [P, P], F32)
-        r0_rest = sb("r0_rest", [P, S - P], F32)
-        r = [None] + [sb("r%d" % t, [P, S], F32) for t in range(1, PACK)]
+        chunks = ((0, 256), (256, 512), (768, 1024), (512, 768))
+        paired = [sb("paired%d" % c, [P, 2, hi - lo], F32) for c, (lo, hi) in enumerate(chunks)]
 
-        for i, (lo, hi) in enumerate(runs):
-            cols = slice(lo * P, hi * P)
-            product(direct[i][:, 0 : (hi - lo) * P], weights(1, 0, 1), tokens(1, lo, hi), 1)
-            nc.vector.tensor_tensor(scaled[i][:], direct[i][:, 0 : (hi - lo) * P], scale_sb[:, cols], MULT)
-            bounded = r0_head[:] if i == 0 else r0_rest[:, (lo - 1) * P : (hi - 1) * P]
-            nc.scalar.activation(bounded, scaled[i][:], TANH)
-        z1 = [sb("z1_%d" % b, [P, P], F32, "stage%d" % (3 - b)) for b in range(BLOCKS)]
-        for b in range(BLOCKS):
-            product(y[b][:, 0:256], tokens(1, b, b + 1), weights(1, 1, 3), 1)
-            nc.scalar.activation(z1[b][:], y[b][:, 0:P], TANH, scale=factor[:, b : b + 1])
-        nc.vector.tensor_copy(window[0][:].indirect(slot_sb[:, 0:per]), r0_head[:])
-        nc.vector.tensor_copy(window[0][:].indirect(slot_sb[:, per : BLOCKS * per]), r0_rest[:])
-        nc.sync.dma_start(out_rows[0], window[0][:])
+        def regroup_and_store(t):
+            for c, (lo, hi) in enumerate(chunks):
+                nc.sync.dma_start(paired[c][64 * t : 64 * (t + 1)], window[t][:, lo:hi])
+            nc.sync.dma_start(rows_of(out_0, t), window[t][:])
 
-        def turn_and_scatter(t, pieces):
-            turned = bank("turned%d" % t, t - 1)
+        regroup_and_store(0)
+
+        y1 = [bank("y1_%d" % b, 4 + b) for b in range(BLOCKS)]
+        for g in range(2):
+            low_products(y1, g, 1)
+        r1 = turn(bound_low(y1, 1), (0,), "r1")
+        scatter(1, 0, BLOCKS, r1[:])
+        regroup_and_store(1)
+
+        z23 = sb("z23", [P, BLOCKS, 2, P], F32)
+        for h in range(2):
+            y23 = bank("y23_%d" % h, (1, 7)[h])
             for b in range(BLOCKS):
-                nc.tensor.transpose(turned[:, b * P : (b + 1) * P], pieces[b], ident[:])
-            nc.scalar.copy(r[t][:], turned[:])
-            nc.vector.tensor_copy(window[t][:].indirect(slot_sb[:]), r[t][:])
-            nc.sync.dma_start(out_rows[t], window[t][:])
-
-        turn_and_scatter(1, [z1[b][:] for b in range(BLOCKS)])
-        z23 = [sb("z23_%d" % b, [P, 2 * P], F32, "stage%d" % (3 - b)) for b in range(BLOCKS)]
-        for b in range(BLOCKS):
-            nc.scalar.activation(z23[b][:, 0:P], y[b][:, P : 2 * P], TANH, scale=factor[:, b : b + 1])
-        y3 = bank("y3last", 3)
-        for b in range(BLOCKS):
-            for g in range(2):
-                product(y3[:, b * P : (b + 1) * P], tokens(g, b, b + 1), weights(g, 3, 4), g)
-        for b in range(BLOCKS):
-            nc.scalar.activation(z23[b][:, P : 2 * P], y3[:, b * P : (b + 1) * P], TANH, scale=factor[:, b : b + 1])
-        turn_and_scatter(2, [z23[b][:, 0:P] for b in range(BLOCKS)])
-        turn_and_scatter(3, [z23[b][:, P : 2 * P] for b in range(BLOCKS)])
+                for g in range(2):
+                    product(y23[:, b * P : (b + 1) * P], tokens(g, b, b + 1), high(g, h, h + 1), g)
+            for b in range(BLOCKS):
+                sums = y23[:, b * P : (b + 1) * P].rearrange("p (m e) -> p e m", e=2)
+                nc.scalar.activation(z23[:, b, :, 64 * h : 64 * (h + 1)], sums, TANH, scale=factor[:, b : b + 1])
+        for t in range(2, PACK):
+            result = turn([z23[:, b, t - 2, :] for b in range(BLOCKS)], (t,), "r%d" % t)
+            scatter(t, 0, BLOCKS, result[:])
+            nc.sync.dma_start(rows_of(out_0, t), window[t][:])
 
         spans = ((0, 512), (512, 768), (768, 1024))
-        woven = [sb("woven%d" % c, [P, hi - lo, PACK], BF16) for c, (lo, hi) in enumerate(spans)]
+        woven = [sb("woven%d" % c, [P, hi - lo, PACK], BF16) for c, (lo, hi) in enumerate(spans[0:2])]
+
+        def weave_pairs(dst, c):
+            nc.scalar.copy(dst[:, :, 0:2], paired[c][:].rearrange("p e c -> p c e"))
+
+        weave_pairs(woven[0][:, 0:256], 0)
+        weave_pairs(woven[0][:, 256:512], 1)
+        weave_pairs(woven[1][:], 3)
+        woven.append(sb("woven2", [P, 256, PACK], BF16, "paired3"))
+        weave_pairs(woven[2][:], 2)
+        nc.scalar.copy(woven[2][:, :, 2], window[2][:, 768:1024])
+        for c in range(2):
+            lo, hi = spans[c]
+            nc.gpsimd.tensor_scalar(woven[c][:, :, 2:4], window[2][:, lo:hi].unsqueeze(2).to_broadcast([P, hi - lo, 2]), 1.0, -0.0, MULT, ADD)
         codes = sb("codes", [P, U], U32)
         plane = sb("plane", [P, U], U8)
-        on_vector = 2
-
-        def spread(t, c, last):
-            lo, hi = spans[c]
-            return woven[c][:, :, t:last], window[t][:, lo:hi].unsqueeze(2).to_broadcast([P, hi - lo, last - t])
-
-        def weave_on_gpsimd(t, c, last):
-            dst, src = spread(t, c, last)
-            nc.gpsimd.tensor_scalar(dst, src, 1.0, -0.0, MULT, mybir.AluOpType.add)
-
-        for c in range(len(spans)):
-            weave_on_gpsimd(0, c, 1)
-        for c in range(len(spans)):
-            weave_on_gpsimd(1, c, PACK)
-        for c in range(on_vector):
-            dst, src = spread(2, c, PACK)
-            nc.scalar.copy(dst, src)
-        weave_on_gpsimd(2, on_vector, PACK)
         for c, (lo, hi) in enumerate(spans):
-            if c == 0:
-                nc.vector.tensor_copy(woven[c][:, 0:320, 3], window[3][:, 0:320])
-                nc.scalar.copy(woven[c][:, 320:hi, 3], window[3][:, 320:hi])
-            elif c == 1:
+            if c < 2:
                 nc.vector.tensor_copy(woven[c][:, :, 3], window[3][:, lo:hi])
             else:
                 nc.scalar.copy(woven[c][:, :, 3], window[3][:, lo:hi])

@@ -62,13 +62,13 @@ def tile_picked_zkvw_tanh_po_kernel(tc, x_words, x_scales, cache, w1, scale, off
         def load_w(g, h):
             nc.sync.dma_start(w_raw[g][h][:], w_rows[g][:, :, h * HALF : (h + 1) * HALF])
 
+        nc.sync.dma_start(xw[0][:].bitcast(I32), words_of(0))
         nc.sync.dma_start(offs_sb[:], offs)
         for q in range(4):
             nc.sync.dma_start(xs[32 * q : 32 * q + 8, :].bitcast(I32), x_scales[:, 4 * q : 4 * q + 4, :].bitcast(I32))
-        nc.sync.dma_start(xw[0][:].bitcast(I32), words_of(0))
-        nc.sync.dma_start(scale_rows[:], scale[0:32, :].rearrange("a (b p) -> (a b) p", p=P))
         nc.sync.dma_start(xw[1][:].bitcast(I32), words_of(1))
         load_w(0, 0)
+        nc.sync.dma_start(scale_rows[:], scale[0:32, :].rearrange("a (b p) -> (a b) p", p=P))
         load_w(1, 0)
         load_w(0, 1)
         nc.sync.dma_start(slot_sb[:], slot)
@@ -78,7 +78,7 @@ def tile_picked_zkvw_tanh_po_kernel(tc, x_words, x_scales, cache, w1, scale, off
 
         xg = [sb("xg%d" % g, [P, S], U32) for g in range(2)]
         sg = sb("sg", [P, S], U8)
-        grouped = [[[sb("grouped%d_%d_%d" % (g, h, u), [P, PACK * P], BF16) for u in range(2)] for h in range(2)] for g in range(2)]
+        grouped = [[[sb("grouped%d_%d_%d" % (g, h, u), [P, PACK * P], BF16) for u in range(1 if (g, h) == (1, 0) else 2)] for h in range(2)] for g in range(2)]
         low_q = [[sb("low_q%d_%d" % (g, h), [P, P], U32) for h in range(2)] for g in range(2)]
         low_s = [[sb("low_s%d_%d" % (g, h), [P, P], U8) for h in range(2)] for g in range(2)]
         high_q = [sb("high_q%d" % g, [P, 2 * P], U32) for g in range(2)]
@@ -141,16 +141,15 @@ def tile_picked_zkvw_tanh_po_kernel(tc, x_words, x_scales, cache, w1, scale, off
         factor = sb("factor", [P, BLOCKS], F32)
         nc.scalar.copy(factor[:], scale_ps[:, 0:BLOCKS])
         y0 = [bank("y0_%d" % b, 4 + b) for b in range(BLOCKS)]
-        deal(0, 0, 0)
+        for g in range(2):
+            deal(g, 0, 0)
+            quantise_w(g, 0, 0)
+            low_products(y0, g, 0)
         deal(0, 0, 1)
-        quantise_w(0, 0, 0)
-        low_products(y0, 0, 0)
-        deal(1, 0, 0, "vector")
-        deal(1, 0, 1)
-        quantise_w(0, 0, 1)
-        quantise_w(1, 0, 0)
-        low_products(y0, 1, 0)
         r0 = turn(bound_low(y0, 0), (0, 1), "r0")
+        grouped[1][0].append(sb("grouped1_0_1", [P, PACK * P], BF16, "grouped1_0_0"))
+        deal(1, 0, 1, "vector")
+        quantise_w(0, 0, 1)
         deal(0, 1, 0, "vector")
         deal(0, 1, 1, "vector")
         quantise_w(1, 0, 1)

@@ -105,8 +105,8 @@ def tile_picked_zkvw_tanh_po_kernel(tc, x_words, x_scales, cache, w1, scale, off
         def tokens(g, lo, hi):
             return xg[g][:, lo * P : hi * P].bitcast(FP8X4), sg[4 * g : P, lo * P : hi * P]
 
-        def product(out, still, moving, g):
-            nc.tensor.matmul_mx(out=out, lhsT=still[0], lhsT_scale=still[1], rhs=moving[0], rhs_scale=moving[1], start=(g == 0), stop=(g == 1))
+        def product(out, still, moving, first, last):
+            nc.tensor.matmul_mx(out=out, lhsT=still[0], lhsT_scale=still[1], rhs=moving[0], rhs_scale=moving[1], start=first, stop=last)
 
         per = P // LIST_ROWS
 
@@ -123,14 +123,11 @@ def tile_picked_zkvw_tanh_po_kernel(tc, x_words, x_scales, cache, w1, scale, off
                 nc.scalar.copy(result[:, i * share * P : (i + 1) * share * P], turned[:, 0 : share * P])
             return result
 
-        def low_products(sums, g, h):
-            for b in range(BLOCKS):
-                product(sums[b][:, 0:P], tokens(g, b, b + 1), low(g, h), g)
 
         def bound_low(sums, h):
             bounded = [sb("z%d_%d" % (h, b), [P, P], F32) for b in range(BLOCKS)]
             for b in range(BLOCKS):
-                nc.scalar.activation(bounded[b][:], sums[b][:, 0:P], TANH, scale=factor[:, b : b + 1])
+                nc.scalar.activation(bounded[b][:], sums[b], TANH, scale=factor[:, b : b + 1])
             return [piece[:] for piece in bounded]
 
         nc.vector.tensor_copy(sg[:], xs[:].indirect(offs_sb[:]))
@@ -144,9 +141,10 @@ def tile_picked_zkvw_tanh_po_kernel(tc, x_words, x_scales, cache, w1, scale, off
         for g in range(2):
             deal(g, 0, 0)
             quantise_w(g, 0, 0)
-            low_products(y0, g, 0)
+            for b in range(BLOCKS):
+                product(y0[b][:, 0:P], tokens(g, b, b + 1), low(g, 0), g == 0, g == 1)
         deal(0, 0, 1)
-        r0 = turn(bound_low(y0, 0), (0, 1), "r0")
+        r0 = turn(bound_low([y0[b][:, 0:P] for b in range(BLOCKS)], 0), (0, 1), "r0")
         grouped[1][0].append(sb("grouped1_0_1", [P, PACK * P], BF16, "grouped1_0_0"))
         deal(1, 0, 1, "vector")
         quantise_w(0, 0, 1)
@@ -171,24 +169,21 @@ def tile_picked_zkvw_tanh_po_kernel(tc, x_words, x_scales, cache, w1, scale, off
 
         regroup_and_store(0)
 
-        y1 = [bank("y1_%d" % b, 4 + b) for b in range(BLOCKS)]
+        y1 = bank("y1", 7)
         for g in range(2):
-            low_products(y1, g, 1)
-        r1 = turn(bound_low(y1, 1), (0,), "r1")
+            for b in range(BLOCKS):
+                product(y1[:, b * P : (b + 1) * P], tokens(g, b, b + 1), low(g, 1), (g, b) == (0, 0), (g, b) == (1, BLOCKS - 1))
+        r1 = turn(bound_low([y1[:, b * P : (b + 1) * P] for b in range(BLOCKS)], 1), (2, 3), "r1")
         scatter(1, 0, BLOCKS, r1[:])
         regroup_and_store(1)
 
-        z23 = sb("z23", [P, BLOCKS, 2, P], F32)
-        for h in range(2):
-            y23 = bank("y23_%d" % h, (1, 7)[h])
-            for b in range(BLOCKS):
-                for g in range(2):
-                    product(y23[:, b * P : (b + 1) * P], tokens(g, b, b + 1), high(g, h, h + 1), g)
-            for b in range(BLOCKS):
-                sums = y23[:, b * P : (b + 1) * P].rearrange("p (m e) -> p e m", e=2)
-                nc.scalar.activation(z23[:, b, :, 64 * h : 64 * (h + 1)], sums, TANH, scale=factor[:, b : b + 1])
+        y23 = [bank("y23_%d" % i, (7, 2)[i]) for i in range(2)]
+        for b in range(BLOCKS):
+            for g in range(2):
+                product(y23[b // 2][:, (b % 2) * 2 * P : (b % 2 + 1) * 2 * P], tokens(g, b, b + 1), high(g, 0, 2), g == 0, g == 1)
         for t in range(2, PACK):
-            result = turn([z23[:, b, t - 2, :] for b in range(BLOCKS)], (t,), "r%d" % t)
+            sums = [y23[b // 2][:, (b % 2) * 2 * P + t - 2 : (b % 2 + 1) * 2 * P : 2] for b in range(BLOCKS)]
+            result = turn(bound_low(sums, t), ((0, 1), (4,))[t - 2], "r%d" % t)
             scatter(t, 0, BLOCKS, result[:])
             nc.sync.dma_start(rows_of(out_0, t), window[t][:])
 

@@ -66,8 +66,8 @@ def tile_picked_zkvw_tanh_po_kernel(tc, x_words, x_scales, cache, w1, scale, off
         nc.sync.dma_start(offs_sb[:], offs)
         for q in range(4):
             nc.sync.dma_start(xs[32 * q : 32 * q + 8, :].bitcast(I32), x_scales[:, 4 * q : 4 * q + 4, :].bitcast(I32))
-        nc.sync.dma_start(xw[1][:].bitcast(I32), words_of(1))
         load_w(0, 0)
+        nc.sync.dma_start(xw[1][:].bitcast(I32), words_of(1))
         nc.sync.dma_start(scale_rows[:], scale[0:32, :].rearrange("a (b p) -> (a b) p", p=P))
         load_w(1, 0)
         load_w(0, 1)
@@ -84,11 +84,13 @@ def tile_picked_zkvw_tanh_po_kernel(tc, x_words, x_scales, cache, w1, scale, off
         high_q = [sb("high_q%d" % g, [P, 2 * P], U32) for g in range(2)]
         high_s = [sb("high_s%d" % g, [P, 2 * P], U8) for g in range(2)]
 
-        def deal(g, h, u, engine="scalar"):
-            src = w_raw[g][h][:].rearrange("p j (l u e) -> p u l j e", u=2, e=2)[:, u]
-            dst = grouped[g][h][u][:].rearrange("p (l e j) -> p l j e", e=2, j=PACK)
+        def deal(g, h, u, engine="scalar", lo=0, hi=64):
+            src = w_raw[g][h][:].rearrange("p j (l u e) -> p u l j e", u=2, e=2)[:, u, lo:hi]
+            dst = grouped[g][h][u][:].rearrange("p (l e j) -> p l j e", e=2, j=PACK)[:, lo:hi]
             if engine == "vector":
                 nc.vector.tensor_copy(dst, src)
+            elif engine == "gpsimd":
+                nc.gpsimd.tensor_scalar(dst.rearrange("p l j e -> p l e j"), src.rearrange("p l j e -> p l e j"), 1.0, -0.0, MULT, ADD)
             else:
                 nc.scalar.copy(dst, src)
 
@@ -131,15 +133,17 @@ def tile_picked_zkvw_tanh_po_kernel(tc, x_words, x_scales, cache, w1, scale, off
             return [piece[:] for piece in bounded]
 
         nc.vector.tensor_copy(sg[:], xs[:].indirect(offs_sb[:]))
-        for g in range(2):
-            nc.vector.tensor_copy(xg[g][:], xw[g][:].indirect(offs_sb[:]))
         scale_ps = bank("scale_ps", 0)
         nc.tensor.transpose(scale_ps[:, 0:P], scale_rows[:], ident[:])
         factor = sb("factor", [P, BLOCKS], F32)
         nc.scalar.copy(factor[:], scale_ps[:, 0:BLOCKS])
         y0 = [bank("y0_%d" % b, 4 + b) for b in range(BLOCKS)]
         for g in range(2):
-            deal(g, 0, 0)
+            nc.vector.tensor_copy(xg[g][:], xw[g][:].indirect(offs_sb[:]))
+            on_gpsimd = (64, 24)[g]
+            deal(g, 0, 0, "gpsimd", 0, on_gpsimd)
+            if on_gpsimd < 64:
+                deal(g, 0, 0, "scalar", on_gpsimd, 64)
             quantise_w(g, 0, 0)
             for b in range(BLOCKS):
                 product(y0[b][:, 0:P], tokens(g, b, b + 1), low(g, 0), g == 0, g == 1)

@@ -78,15 +78,19 @@ def tile_picked_zkvw_tanh_po_kernel(tc, x_words, x_scales, cache, w1, scale, off
 
         xg = [sb("xg%d" % g, [P, S], U32) for g in range(2)]
         sg = sb("sg", [P, S], U8)
-        grouped = [[[sb("grouped%d_%d_%d" % (g, h, u), [P, PACK * P], BF16) for u in range(1 if (g, h) == (1, 0) else 2)] for h in range(2)] for g in range(2)]
+        low_in = [[sb("low_in%d_%d" % (g, h), [P, PACK * P], BF16) for h in range(2)] for g in range(2)]
+        high_in = [sb("high_in0", [P, 2 * PACK * P], BF16)]
         low_q = [[sb("low_q%d_%d" % (g, h), [P, P], U32) for h in range(2)] for g in range(2)]
         low_s = [[sb("low_s%d_%d" % (g, h), [P, P], U8) for h in range(2)] for g in range(2)]
         high_q = [sb("high_q%d" % g, [P, 2 * P], U32) for g in range(2)]
         high_s = [sb("high_s%d" % g, [P, 2 * P], U8) for g in range(2)]
 
-        def deal(g, h, u, engine="scalar", lo=0, hi=64):
-            src = w_raw[g][h][:].rearrange("p j (l u e) -> p u l j e", u=2, e=2)[:, u, lo:hi]
-            dst = grouped[g][h][u][:].rearrange("p (l e j) -> p l j e", e=2, j=PACK)[:, lo:hi]
+        def columns(g, h, u):
+            return w_raw[g][h][:].rearrange("p j (l u e) -> p u l j e", u=2, e=2)[:, u]
+
+        def deal_low(g, h, engine, lo=0, hi=64):
+            src = columns(g, h, 0)[:, lo:hi]
+            dst = low_in[g][h][:].rearrange("p (l e j) -> p l j e", e=2, j=PACK)[:, lo:hi]
             if engine == "vector":
                 nc.vector.tensor_copy(dst, src)
             elif engine == "gpsimd":
@@ -94,15 +98,23 @@ def tile_picked_zkvw_tanh_po_kernel(tc, x_words, x_scales, cache, w1, scale, off
             else:
                 nc.scalar.copy(dst, src)
 
-        def low(g, h):
-            return low_q[g][h][:].bitcast(FP8X4), low_s[g][h][:]
+        def deal_high(g, h, engine):
+            dst = high_in[g][:].rearrange("p (e h l j) -> p h l j e", e=2, h=2, j=PACK)[:, h]
+            if engine == "vector":
+                nc.vector.tensor_copy(dst, columns(g, h, 1))
+            else:
+                nc.scalar.copy(dst, columns(g, h, 1))
 
-        def high(g, first, last):
-            return high_q[g][:, first * P : last * P].bitcast(FP8X4), high_s[g][:, first * P : last * P]
+        def weights(t, g):
+            if t < 2:
+                return low_q[g][t][:].bitcast(FP8X4), low_s[g][t][:]
+            return high_q[g][:, (t - 2) * P : (t - 1) * P].bitcast(FP8X4), high_s[g][:, (t - 2) * P : (t - 1) * P]
 
-        def quantise_w(g, h, u):
-            codes, scales = low(g, h) if u == 0 else high(g, h, h + 1)
-            nc.vector.quantize_mx(out=codes, scales=scales, in_=grouped[g][h][u][:])
+        def quantise_low(g, h):
+            nc.vector.quantize_mx(out=low_q[g][h][:].bitcast(FP8X4), scales=low_s[g][h][:], in_=low_in[g][h][:])
+
+        def quantise_high(g):
+            nc.vector.quantize_mx(out=high_q[g][:].bitcast(FP8X4), scales=high_s[g][:], in_=high_in[g][:])
 
         def tokens(g, lo, hi):
             return xg[g][:, lo * P : hi * P].bitcast(FP8X4), sg[4 * g : P, lo * P : hi * P]
@@ -141,26 +153,21 @@ def tile_picked_zkvw_tanh_po_kernel(tc, x_words, x_scales, cache, w1, scale, off
         for g in range(2):
             nc.vector.tensor_copy(xg[g][:], xw[g][:].indirect(offs_sb[:]))
             on_gpsimd = (64, 24)[g]
-            deal(g, 0, 0, "gpsimd", 0, on_gpsimd)
+            deal_low(g, 0, "gpsimd", 0, on_gpsimd)
             if on_gpsimd < 64:
-                deal(g, 0, 0, "scalar", on_gpsimd, 64)
-            quantise_w(g, 0, 0)
+                deal_low(g, 0, "scalar", on_gpsimd, 64)
+            quantise_low(g, 0)
             for b in range(BLOCKS):
-                product(y0[b][:, 0:P], tokens(g, b, b + 1), low(g, 0), g == 0, g == 1)
-        deal(0, 0, 1)
+                product(y0[b][:, 0:P], tokens(g, b, b + 1), weights(0, g), g == 0, g == 1)
+        deal_high(0, 0, "scalar")
         r0 = turn(bound_low([y0[b][:, 0:P] for b in range(BLOCKS)], 0), (0, 1), "r0")
-        grouped[1][0].append(sb("grouped1_0_1", [P, PACK * P], BF16, "grouped1_0_0"))
-        deal(1, 0, 1, "vector")
-        quantise_w(0, 0, 1)
-        deal(0, 1, 0, "vector")
-        deal(0, 1, 1, "vector")
-        quantise_w(1, 0, 1)
-        quantise_w(0, 1, 0)
-        quantise_w(0, 1, 1)
-        deal(1, 1, 0, "vector")
-        deal(1, 1, 1, "vector")
-        quantise_w(1, 1, 0)
-        quantise_w(1, 1, 1)
+        high_in.append(sb("high_in1", [P, 2 * PACK * P], BF16, "low_in1_0"))
+        deal_high(1, 0, "vector")
+        for g in range(2):
+            deal_low(g, 1, "vector")
+            deal_high(g, 1, "vector")
+            quantise_low(g, 1)
+            quantise_high(g)
         scatter(0, 0, BLOCKS, r0[:])
 
         chunks = ((0, 256), (256, 512), (768, 1024), (512, 768))
@@ -173,23 +180,17 @@ def tile_picked_zkvw_tanh_po_kernel(tc, x_words, x_scales, cache, w1, scale, off
 
         regroup_and_store(0)
 
-        y1 = bank("y1", 7)
-        for g in range(2):
-            for b in range(BLOCKS):
-                product(y1[:, b * P : (b + 1) * P], tokens(g, b, b + 1), low(g, 1), (g, b) == (0, 0), (g, b) == (1, BLOCKS - 1))
-        r1 = turn(bound_low([y1[:, b * P : (b + 1) * P] for b in range(BLOCKS)], 1), (2, 3), "r1")
-        scatter(1, 0, BLOCKS, r1[:])
-        regroup_and_store(1)
-
-        y23 = [bank("y23_%d" % i, (7, 2)[i]) for i in range(2)]
-        for b in range(BLOCKS):
+        for t in range(1, PACK):
+            sums = bank("y%d" % t, 7)
             for g in range(2):
-                product(y23[b // 2][:, (b % 2) * 2 * P : (b % 2 + 1) * 2 * P], tokens(g, b, b + 1), high(g, 0, 2), g == 0, g == 1)
-        for t in range(2, PACK):
-            sums = [y23[b // 2][:, (b % 2) * 2 * P + t - 2 : (b % 2 + 1) * 2 * P : 2] for b in range(BLOCKS)]
-            result = turn(bound_low(sums, t), ((0, 1), (4,))[t - 2], "r%d" % t)
+                for b in range(BLOCKS):
+                    product(sums[:, b * P : (b + 1) * P], tokens(g, b, b + 1), weights(t, g), (g, b) == (0, 0), (g, b) == (1, BLOCKS - 1))
+            result = turn(bound_low([sums[:, b * P : (b + 1) * P] for b in range(BLOCKS)], t), ((2, 3), (0, 1), (2, 3))[t - 1], "r%d" % t)
             scatter(t, 0, BLOCKS, result[:])
-            nc.sync.dma_start(rows_of(out_0, t), window[t][:])
+            if t == 1:
+                regroup_and_store(t)
+            else:
+                nc.sync.dma_start(rows_of(out_0, t), window[t][:])
 
         spans = ((0, 512), (512, 768), (768, 1024))
         woven = [sb("woven%d" % c, [P, hi - lo, PACK], BF16) for c, (lo, hi) in enumerate(spans[0:2])]

@@ -171,11 +171,13 @@ def tile_picked_zkvw_tanh_po_kernel(tc, x_words, x_scales, cache, w1, scale, off
         scatter(0, 0, BLOCKS, r0[:])
 
         chunks = ((0, 256), (256, 512), (768, 1024), (512, 768))
-        paired = [sb("paired%d" % c, [P, 2, hi - lo], F32) for c, (lo, hi) in enumerate(chunks)]
+        paired = [sb("paired%d" % c, [P, 2, hi - lo], BF16) for c, (lo, hi) in enumerate(chunks)]
 
         def regroup_and_store(t):
             for c, (lo, hi) in enumerate(chunks):
-                nc.sync.dma_start(paired[c][64 * t : 64 * (t + 1)], window[t][:, lo:hi])
+                rounded = sb("rounded%d_%d" % (t, c), [P, hi - lo], BF16)
+                nc.gpsimd.tensor_scalar(rounded[:], window[t][:, lo:hi], 1.0, -0.0, MULT, ADD)
+                nc.sync.dma_start(paired[c][64 * t : 64 * (t + 1)], rounded[:])
             nc.sync.dma_start(rows_of(out_0, t), window[t][:])
 
         regroup_and_store(0)

@@ -1,7 +1,6 @@
 from contextlib import ExitStack
 
 import concourse.mybir as mybir
-from concourse.masks import make_identity
 
 K, T, S, N, U = 1024, 1024, 512, 512, 1024
 FLOPS = 2 * K * N * S
@@ -14,14 +13,18 @@ U16 = mybir.dt.uint16
 U8 = mybir.dt.uint8
 FP8X4 = mybir.dt.float8_e4m3fn_x4
 TANH = mybir.ActivationFunctionType.Tanh
+COPY = mybir.ActivationFunctionType.Copy
 MULT = mybir.AluOpType.mult
 ADD = mybir.AluOpType.add
 
 P = 128
 PACK = 4
+PASSES = 2
 LIST_ROWS = 16
-BLOCKS = S // P
 HALF = N // 2
+WORDS = P // 2
+CHUNK = 256
+ON_VECTOR = 40
 
 
 def tile_picked_zkvw_tanh_po_kernel(tc, x_words, x_scales, cache, w1, scale, offs, slot, out_0, out_1, out_2):
@@ -33,192 +36,138 @@ def tile_picked_zkvw_tanh_po_kernel(tc, x_words, x_scales, cache, w1, scale, off
         def sb(name, shape, dtype, tag=None):
             return held.tile(shape, dtype, name=name, tag=tag or name, align_bytes=64)
 
-        def bank(name, index):
-            return psum.tile([P, 512], F32, name=name, tag="bank%d" % index)
-
         offs_sb = sb("offs_sb", [P, S // LIST_ROWS], U16)
         slot_sb = sb("slot_sb", [P, S // LIST_ROWS], U16)
-        xw = [sb("xw%d" % g, [P, T], U32) for g in range(2)]
+        xw = [sb("xw%d" % g, [P, T], U32) for g in range(PASSES)]
         xs = sb("xs", [P, T], U8)
-        w_raw = [[sb("w_raw%d_%d" % (g, h), [P, PACK, HALF], F32) for h in range(2)] for g in range(2)]
-        scale_rows = sb("scale_rows", [P, P], F32)
+        w_raw = [[sb("w_raw%d_%d" % (g, h), [P, PACK, HALF], F32) for h in range(2)] for g in range(PASSES)]
+        scale_sb = sb("scale_sb", [P, S], F32)
         window = [sb("window%d" % t, [P, U], F32) for t in range(PACK)]
-        ident = sb("ident", [P, P], F32)
 
         nc.gpsimd.memset(xs[:].bitcast(I32), 0)
-        make_identity(nc, ident[:])
 
-        def words_of(g):
-            return x_words[g].rearrange("p c r -> p (c r)").bitcast(I32)
+        w_rows = w1.rearrange("(g p j) n -> g p j n", g=PASSES, j=PACK)
 
-        w_rows = w1.rearrange("(g p j) n -> g p j n", g=2, j=PACK)
+        def load_x(g):
+            nc.sync.dma_start(xw[g][:].bitcast(I32), x_words[g].rearrange("p c r -> p (c r)").bitcast(I32))
 
-        def rows_of(matrix, t):
-            by_word = matrix.rearrange("(l r) c -> l r c", r=PACK)
-            if t < 2:
-                return by_word[64 * t : 64 * (t + 1), 0:2, :]
-            return by_word[:, t, :]
+        def load_w(g):
+            for h in range(2):
+                nc.sync.dma_start(w_raw[g][h][:], w_rows[g][:, :, h * HALF : (h + 1) * HALF])
 
-        def load_w(g, h):
-            nc.sync.dma_start(w_raw[g][h][:], w_rows[g][:, :, h * HALF : (h + 1) * HALF])
+        def plane_of(matrix, t):
+            return matrix.rearrange("(l r) c -> l r c", r=PACK)[:, t, :]
 
-        nc.sync.dma_start(xw[0][:].bitcast(I32), words_of(0))
+        load_x(0)
         nc.sync.dma_start(offs_sb[:], offs)
         for q in range(4):
             nc.sync.dma_start(xs[32 * q : 32 * q + 8, :].bitcast(I32), x_scales[:, 4 * q : 4 * q + 4, :].bitcast(I32))
-        load_w(0, 0)
-        nc.sync.dma_start(xw[1][:].bitcast(I32), words_of(1))
-        nc.sync.dma_start(scale_rows[:], scale[0:32, :].rearrange("a (b p) -> (a b) p", p=P))
-        load_w(1, 0)
-        load_w(0, 1)
+        load_w(0)
+        load_x(1)
+        load_w(1)
+        nc.sync.dma_start(scale_sb[:], scale)
         nc.sync.dma_start(slot_sb[:], slot)
-        load_w(1, 1)
         for t in range(PACK):
-            nc.sync.dma_start(window[t][:], rows_of(cache, t))
+            nc.sync.dma_start(window[t][:], plane_of(cache, t))
 
-        xg = [sb("xg%d" % g, [P, S], U32) for g in range(2)]
+        xg = [sb("xg%d" % g, [P, S], U32) for g in range(PASSES)]
         sg = sb("sg", [P, S], U8)
-        low_in = [[sb("low_in%d_%d" % (g, h), [P, PACK * P], BF16) for h in range(2)] for g in range(2)]
-        high_in = [sb("high_in0", [P, 2 * PACK * P], BF16)]
-        low_q = [[sb("low_q%d_%d" % (g, h), [P, P], U32) for h in range(2)] for g in range(2)]
-        low_s = [[sb("low_s%d_%d" % (g, h), [P, P], U8) for h in range(2)] for g in range(2)]
-        high_q = [sb("high_q%d" % g, [P, 2 * P], U32) for g in range(2)]
-        high_s = [sb("high_s%d" % g, [P, 2 * P], U8) for g in range(2)]
+        dealt = [sb("dealt%d" % g, [P, PACK, P, PACK], BF16) for g in range(PASSES)]
+        w_q = [[sb("w_q%d_%d" % (g, t), [P, P], U32) for t in range(PACK)] for g in range(PASSES)]
+        w_s = [[sb("w_s%d_%d" % (g, t), [P, P], U8) for t in range(PACK)] for g in range(PASSES)]
+        sums = [psum.tile([P, S], F32, name="sums%d" % t, tag="sums%d" % t) for t in range(PACK)]
 
-        def columns(g, h, u):
-            return w_raw[g][h][:].rearrange("p j (l u e) -> p u l j e", u=2, e=2)[:, u]
-
-        def deal_low(g, h, engine, lo=0, hi=64):
-            src = columns(g, h, 0)[:, lo:hi]
-            dst = low_in[g][h][:].rearrange("p (l e j) -> p l j e", e=2, j=PACK)[:, lo:hi]
+        def deal(g, h, engine, lo, hi):
+            src = w_raw[g][h][:].rearrange("p j (l t) -> p l t j", t=PACK)[:, lo:hi]
+            dst = dealt[g][:].rearrange("p t l j -> p l t j")[:, h * WORDS + lo : h * WORDS + hi]
             if engine == "vector":
                 nc.vector.tensor_copy(dst, src)
             elif engine == "gpsimd":
-                nc.gpsimd.tensor_scalar(dst.rearrange("p l j e -> p l e j"), src.rearrange("p l j e -> p l e j"), 1.0, -0.0, MULT, ADD)
+                nc.gpsimd.tensor_scalar(dst, src, 1.0, -0.0, MULT, ADD)
             else:
                 nc.scalar.copy(dst, src)
 
-        def deal_high(g, h, engine):
-            dst = high_in[g][:].rearrange("p (e h l j) -> p h l j e", e=2, h=2, j=PACK)[:, h]
-            if engine == "vector":
-                nc.vector.tensor_copy(dst, columns(g, h, 1))
-            else:
-                nc.scalar.copy(dst, columns(g, h, 1))
-
-        def weights(t, g):
-            if t < 2:
-                return low_q[g][t][:].bitcast(FP8X4), low_s[g][t][:]
-            return high_q[g][:, (t - 2) * P : (t - 1) * P].bitcast(FP8X4), high_s[g][:, (t - 2) * P : (t - 1) * P]
-
-        def quantise_low(g, h):
-            nc.vector.quantize_mx(out=low_q[g][h][:].bitcast(FP8X4), scales=low_s[g][h][:], in_=low_in[g][h][:])
-
-        def quantise_high(g):
-            nc.vector.quantize_mx(out=high_q[g][:].bitcast(FP8X4), scales=high_s[g][:], in_=high_in[g][:])
-
-        def tokens(g, lo, hi):
-            return xg[g][:, lo * P : hi * P].bitcast(FP8X4), sg[4 * g : P, lo * P : hi * P]
-
-        def product(out, still, moving, first, last):
-            nc.tensor.matmul_mx(out=out, lhsT=still[0], lhsT_scale=still[1], rhs=moving[0], rhs_scale=moving[1], start=first, stop=last)
-
-        per = P // LIST_ROWS
-
-        def scatter(t, lo, hi, values):
-            nc.vector.tensor_copy(window[t][:].indirect(slot_sb[:, lo * per : hi * per]), values)
-
-        def turn(pieces, banks, name):
-            result = sb(name, [P, S], F32)
-            share = BLOCKS // len(banks)
-            for i, index in enumerate(banks):
-                turned = bank("turned_%s_%d" % (name, i), index)
-                for b in range(share):
-                    nc.tensor.transpose(turned[:, b * P : (b + 1) * P], pieces[i * share + b], ident[:])
-                nc.scalar.copy(result[:, i * share * P : (i + 1) * share * P], turned[:, 0 : share * P])
-            return result
-
-
-        def bound_low(sums, h):
-            bounded = [sb("z%d_%d" % (h, b), [P, P], F32) for b in range(BLOCKS)]
-            for b in range(BLOCKS):
-                nc.scalar.activation(bounded[b][:], sums[b], TANH, scale=factor[:, b : b + 1])
-            return [piece[:] for piece in bounded]
+        def quantise_and_multiply(g):
+            for t in range(PACK):
+                nc.vector.quantize_mx(out=w_q[g][t][:].bitcast(FP8X4), scales=w_s[g][t][:], in_=dealt[g][:, t].rearrange("p l j -> p (l j)"))
+            for t in range(PACK):
+                nc.tensor.matmul_mx(out=sums[t][:], lhsT=w_q[g][t][:].bitcast(FP8X4), lhsT_scale=w_s[g][t][:], rhs=xg[g][:].bitcast(FP8X4), rhs_scale=sg[4 * g : P, :], start=g == 0, stop=g == PASSES - 1)
 
         nc.vector.tensor_copy(sg[:], xs[:].indirect(offs_sb[:]))
-        scale_ps = bank("scale_ps", 0)
-        nc.tensor.transpose(scale_ps[:, 0:P], scale_rows[:], ident[:])
-        factor = sb("factor", [P, BLOCKS], F32)
-        nc.scalar.copy(factor[:], scale_ps[:, 0:BLOCKS])
-        y0 = [bank("y0_%d" % b, 4 + b) for b in range(BLOCKS)]
-        for g in range(2):
-            nc.vector.tensor_copy(xg[g][:], xw[g][:].indirect(offs_sb[:]))
-            on_gpsimd = (64, 24)[g]
-            deal_low(g, 0, "gpsimd", 0, on_gpsimd)
-            if on_gpsimd < 64:
-                deal_low(g, 0, "scalar", on_gpsimd, 64)
-            quantise_low(g, 0)
-            for b in range(BLOCKS):
-                product(y0[b][:, 0:P], tokens(g, b, b + 1), weights(0, g), g == 0, g == 1)
-        deal_high(0, 0, "scalar")
-        r0 = turn(bound_low([y0[b][:, 0:P] for b in range(BLOCKS)], 0), (0, 1), "r0")
-        high_in.append(sb("high_in1", [P, 2 * PACK * P], BF16, "low_in1_0"))
-        deal_high(1, 0, "vector")
-        for g in range(2):
-            deal_low(g, 1, "vector")
-            deal_high(g, 1, "vector")
-            quantise_low(g, 1)
-            quantise_high(g)
-        scatter(0, 0, BLOCKS, r0[:])
+        nc.vector.tensor_copy(xg[0][:], xw[0][:].indirect(offs_sb[:]))
+        deal(0, 0, "scalar", 0, WORDS)
+        deal(0, 1, "scalar", 0, WORDS // 2)
+        deal(0, 1, "gpsimd", WORDS // 2, WORDS)
+        quantise_and_multiply(0)
+        nc.vector.tensor_copy(xg[1][:], xw[1][:].indirect(offs_sb[:]))
+        deal(1, 0, "scalar", 0, WORDS)
+        deal(1, 1, "vector", 0, ON_VECTOR)
+        deal(1, 1, "scalar", ON_VECTOR, WORDS)
+        quantise_and_multiply(1)
 
-        chunks = ((0, 256), (256, 512), (768, 1024), (512, 768))
-        paired = [sb("paired%d" % c, [P, 2, hi - lo], BF16) for c, (lo, hi) in enumerate(chunks)]
+        scaled = [sb("scaled%d" % t, [P, S], F32) for t in range(PACK)]
+        bounded = [sb("bounded%d" % t, [P, S], F32) for t in range(PACK)]
+        for t in range(PACK):
+            nc.vector.tensor_tensor(scaled[t][:], sums[t][:], scale_sb[:], MULT)
 
-        def regroup_and_store(t):
-            for c, (lo, hi) in enumerate(chunks):
-                rounded = sb("rounded%d_%d" % (t, c), [P, hi - lo], BF16)
-                nc.gpsimd.tensor_scalar(rounded[:], window[t][:, lo:hi], 1.0, -0.0, MULT, ADD)
-                nc.sync.dma_start(paired[c][64 * t : 64 * (t + 1)], rounded[:])
-            nc.sync.dma_start(rows_of(out_0, t), window[t][:])
+        def bound(t):
+            nc.scalar.activation(bounded[t][:], scaled[t][:], TANH)
 
-        regroup_and_store(0)
-
-        for t in range(1, PACK):
-            sums = bank("y%d" % t, 7)
-            for g in range(2):
-                for b in range(BLOCKS):
-                    product(sums[:, b * P : (b + 1) * P], tokens(g, b, b + 1), weights(t, g), (g, b) == (0, 0), (g, b) == (1, BLOCKS - 1))
-            result = turn(bound_low([sums[:, b * P : (b + 1) * P] for b in range(BLOCKS)], t), ((2, 3), (0, 1), (2, 3))[t - 1], "r%d" % t)
-            scatter(t, 0, BLOCKS, result[:])
-            if t == 1:
-                regroup_and_store(t)
+        def scatter(engine, t, lo, hi):
+            target = window[t][:].indirect(slot_sb[:, lo // LIST_ROWS : hi // LIST_ROWS])
+            if engine == "vector":
+                nc.vector.tensor_copy(target, bounded[t][:, lo:hi])
             else:
-                nc.sync.dma_start(rows_of(out_0, t), window[t][:])
+                nc.scalar.activation(target, bounded[t][:, lo:hi], COPY)
 
-        spans = ((0, 512), (512, 768), (768, 1024))
-        woven = [sb("woven%d" % c, [P, hi - lo, PACK], BF16) for c, (lo, hi) in enumerate(spans[0:2])]
+        def store(t):
+            nc.sync.dma_start(plane_of(out_0, t), window[t][:])
 
-        def weave_pairs(dst, c):
-            nc.scalar.copy(dst[:, :, 0:2], paired[c][:].rearrange("p e c -> p c e"))
+        chunks = U // CHUNK
+        pairs = [sb("pairs%d" % c, [P, 2, CHUNK, 2], BF16) for c in range(chunks)]
 
-        weave_pairs(woven[0][:, 0:256], 0)
-        weave_pairs(woven[0][:, 256:512], 1)
-        weave_pairs(woven[1][:], 3)
-        woven.append(sb("woven2", [P, 256, PACK], BF16, "paired3"))
-        weave_pairs(woven[2][:], 2)
-        nc.scalar.copy(woven[2][:, :, 2], window[2][:, 768:1024])
-        for c in range(2):
-            lo, hi = spans[c]
-            nc.gpsimd.tensor_scalar(woven[c][:, :, 2:4], window[2][:, lo:hi].unsqueeze(2).to_broadcast([P, hi - lo, 2]), 1.0, -0.0, MULT, ADD)
+        def cols(t, c):
+            return window[t][:, c * CHUNK : (c + 1) * CHUNK]
+
+        bound(0)
+        bound(1)
+        scatter("scalar", 0, 0, S // 2)
+        bound(2)
+        scatter("vector", 1, 0, S)
+        scatter("scalar", 0, S // 2, S)
+        store(0)
+        store(1)
+        bound(3)
+        for t in range(2):
+            for c in range(chunks):
+                nc.gpsimd.tensor_scalar(pairs[c][:, 0, :, t], cols(t, c), 1.0, -0.0, MULT, ADD)
+        scatter("vector", 2, 0, S)
+        scatter("scalar", 3, 0, S // 2)
+        scatter("scalar", 3, S // 2, S)
+        store(2)
+        store(3)
+
+        on_vector = chunks // 2
+        for c in range(chunks):
+            if c < on_vector:
+                nc.vector.tensor_copy(pairs[c][:, 1, :, 0], cols(2, c))
+            else:
+                nc.vector.tensor_copy(pairs[c][:, 1], cols(2, c).unsqueeze(2).to_broadcast([P, CHUNK, 2]))
+        woven = [sb("woven%d" % c, [P, CHUNK, 2], F32) for c in range(chunks)]
+        for c in range(chunks):
+            if c < on_vector:
+                nc.vector.tensor_copy(pairs[c][:, 1, :, 1], cols(3, c))
+            else:
+                nc.scalar.copy(pairs[c][:, 1, :, 1], cols(3, c))
+                nc.scalar.copy(woven[c][:], pairs[c][:].rearrange("p u c e -> p (u c e)").bitcast(F32).rearrange("p (u c) -> p c u", u=2))
+        for c in range(on_vector):
+            nc.vector.tensor_copy(woven[c][:], pairs[c][:].rearrange("p u c e -> p (u c e)").bitcast(F32).rearrange("p (u c) -> p c u", u=2))
         codes = sb("codes", [P, U], U32)
         plane = sb("plane", [P, U], U8)
-        for c, (lo, hi) in enumerate(spans):
-            if c < 2:
-                nc.vector.tensor_copy(woven[c][:, :, 3], window[3][:, lo:hi])
-            else:
-                nc.scalar.copy(woven[c][:, :, 3], window[3][:, lo:hi])
         out_words = out_1[0].rearrange("p c r -> p (c r)").bitcast(I32)
-        for c, (lo, hi) in enumerate(spans):
-            nc.vector.quantize_mx(out=codes[:, lo:hi].bitcast(FP8X4), scales=plane[:, lo:hi], in_=woven[c][:].rearrange("p c t -> p (c t)"))
+        for c in range(chunks):
+            lo, hi = c * CHUNK, (c + 1) * CHUNK
+            nc.vector.quantize_mx(out=codes[:, lo:hi].bitcast(FP8X4), scales=plane[:, lo:hi], in_=woven[c][:].rearrange("p c u -> p (c u)").bitcast(BF16))
             nc.sync.dma_start(out_words[:, lo:hi], codes[:, lo:hi].bitcast(I32))
         for q in range(4):
             queue = nc.sync if q == 0 else nc.scalar

@@ -23,7 +23,6 @@ PASSES = 2
 LIST_ROWS = 16
 HALF = N // 2
 WORDS = P // 2
-CHUNK = 256
 ON_VECTOR = 40
 
 
@@ -67,15 +66,16 @@ def tile_picked_zkvw_tanh_po_kernel(tc, x_words, x_scales, cache, w1, scale, off
         load_w(1)
         nc.sync.dma_start(scale_sb[:], scale)
         nc.sync.dma_start(slot_sb[:], slot)
-        for t in range(PACK):
-            nc.sync.dma_start(window[t][:], plane_of(cache, t))
+        for t, lo, hi in ((0, 0, U), (1, 0, U), (2, 0, 768), (3, 0, U), (2, 768, U)):
+            nc.sync.dma_start(window[t][:, lo:hi], plane_of(cache, t)[:, lo:hi])
 
-        xg = [sb("xg%d" % g, [P, S], U32) for g in range(PASSES)]
+        xg = [sb("xg0", [P, S], U32)]
         sg = sb("sg", [P, S], U8)
         dealt = [sb("dealt%d" % g, [P, PACK, P, PACK], BF16) for g in range(PASSES)]
         w_q = [[sb("w_q%d_%d" % (g, t), [P, P], U32) for t in range(PACK)] for g in range(PASSES)]
         w_s = [[sb("w_s%d_%d" % (g, t), [P, P], U8) for t in range(PACK)] for g in range(PASSES)]
-        sums = [psum.tile([P, S], F32, name="sums%d" % t, tag="sums%d" % t) for t in range(PACK)]
+        pieces = ((1, 0, S // 2), (0, 0, S // 2), (1, S // 2, S), (0, S // 2, S), (2, 0, S), (3, 0, S))
+        sums = [psum.tile([P, hi - lo], F32, name="sums%d" % i, tag="sums%d" % i) for i, (t, lo, hi) in enumerate(pieces)]
 
         def deal(g, h, engine, lo, hi):
             src = w_raw[g][h][:].rearrange("p j (l t) -> p l t j", t=PACK)[:, lo:hi]
@@ -88,10 +88,10 @@ def tile_picked_zkvw_tanh_po_kernel(tc, x_words, x_scales, cache, w1, scale, off
                 nc.scalar.copy(dst, src)
 
         def quantise_and_multiply(g):
-            for t in range(PACK):
+            for t in (1, 0, 2, 3):
                 nc.vector.quantize_mx(out=w_q[g][t][:].bitcast(FP8X4), scales=w_s[g][t][:], in_=dealt[g][:, t].rearrange("p l j -> p (l j)"))
-            for t in range(PACK):
-                nc.tensor.matmul_mx(out=sums[t][:], lhsT=w_q[g][t][:].bitcast(FP8X4), lhsT_scale=w_s[g][t][:], rhs=xg[g][:].bitcast(FP8X4), rhs_scale=sg[4 * g : P, :], start=g == 0, stop=g == PASSES - 1)
+            for i, (t, lo, hi) in enumerate(pieces):
+                nc.tensor.matmul_mx(out=sums[i][:], lhsT=w_q[g][t][:].bitcast(FP8X4), lhsT_scale=w_s[g][t][:], rhs=xg[g][:, lo:hi].bitcast(FP8X4), rhs_scale=sg[4 * g : P, lo:hi], start=g == 0, stop=g == PASSES - 1)
 
         nc.vector.tensor_copy(sg[:], xs[:].indirect(offs_sb[:]))
         nc.vector.tensor_copy(xg[0][:], xw[0][:].indirect(offs_sb[:]))
@@ -99,74 +99,91 @@ def tile_picked_zkvw_tanh_po_kernel(tc, x_words, x_scales, cache, w1, scale, off
         deal(0, 1, "scalar", 0, WORDS // 2)
         deal(0, 1, "gpsimd", WORDS // 2, WORDS)
         quantise_and_multiply(0)
+        xg.append(sb("xg1", [P, S], U32, "dealt0"))
         nc.vector.tensor_copy(xg[1][:], xw[1][:].indirect(offs_sb[:]))
         deal(1, 0, "scalar", 0, WORDS)
         deal(1, 1, "vector", 0, ON_VECTOR)
         deal(1, 1, "scalar", ON_VECTOR, WORDS)
         quantise_and_multiply(1)
 
-        scaled = [sb("scaled%d" % t, [P, S], F32) for t in range(PACK)]
-        bounded = [sb("bounded%d" % t, [P, S], F32) for t in range(PACK)]
-        for t in range(PACK):
-            nc.vector.tensor_tensor(scaled[t][:], sums[t][:], scale_sb[:], MULT)
+        scaled = [sb("scaled%d" % i, [P, hi - lo], F32) for i, (t, lo, hi) in enumerate(pieces)]
+        for i, (t, lo, hi) in enumerate(pieces):
+            nc.vector.tensor_tensor(scaled[i][:], sums[i][:], scale_sb[:, lo:hi], MULT)
 
-        def bound(t):
-            nc.scalar.activation(bounded[t][:], scaled[t][:], TANH)
+        early = sb("early", [P, S // 2], F32)
+        whole = sb("whole", [P, S], F32)
+        late = sb("late", [P, S // 2 + S], F32, "scale_sb")
+        last = sb("last", [P, S], F32)
+
+        def bounded(t, lo, hi):
+            if t == 0:
+                return early[:, lo:hi] if hi <= S // 2 else late[:, lo - S // 2 : hi - S // 2]
+            if t == 2:
+                return late[:, S // 2 + lo : S // 2 + hi]
+            return (whole if t == 1 else last)[:, lo:hi]
+
+        def bound(i):
+            nc.scalar.activation(bounded(*pieces[i]), scaled[i][:], TANH)
 
         def scatter(engine, t, lo, hi):
             target = window[t][:].indirect(slot_sb[:, lo // LIST_ROWS : hi // LIST_ROWS])
             if engine == "vector":
-                nc.vector.tensor_copy(target, bounded[t][:, lo:hi])
+                nc.vector.tensor_copy(target, bounded(t, lo, hi))
             else:
-                nc.scalar.activation(target, bounded[t][:, lo:hi], COPY)
+                nc.scalar.activation(target, bounded(t, lo, hi), COPY)
 
         def store(t):
             nc.sync.dma_start(plane_of(out_0, t), window[t][:])
 
-        chunks = U // CHUNK
-        pairs = [sb("pairs%d" % c, [P, 2, CHUNK, 2], BF16) for c in range(chunks)]
+        spans = ((0, 256, "vector"), (256, 512, "vector"), (512, 896, "scalar"), (896, 1024, "scalar"))
+        pairs = [sb("pairs%d" % c, [P, 2, hi - lo, 2], BF16) for c, (lo, hi, engine) in enumerate(spans)]
+        woven = [sb("woven%d" % c, [P, hi - lo, 2], F32) for c, (lo, hi, engine) in enumerate(spans)]
 
-        def cols(t, c):
-            return window[t][:, c * CHUNK : (c + 1) * CHUNK]
+        def place(t, c):
+            lo, hi, engine = spans[c]
+            dst, src = pairs[c][:, t // 2, :, t % 2], window[t][:, lo:hi]
+            if t < 2:
+                nc.gpsimd.tensor_scalar(dst, src, 1.0, -0.0, MULT, ADD)
+            elif engine == "vector":
+                nc.vector.tensor_copy(dst, src)
+            else:
+                nc.scalar.copy(dst, src)
+
+        def weave(c):
+            src = pairs[c][:].rearrange("p u c e -> p (u c e)").bitcast(F32).rearrange("p (u c) -> p c u", u=2)
+            if spans[c][2] == "vector":
+                nc.vector.tensor_copy(woven[c][:], src)
+            else:
+                nc.scalar.copy(woven[c][:], src)
 
         bound(0)
         bound(1)
-        scatter("scalar", 0, 0, S // 2)
         bound(2)
+        scatter("scalar", 0, 0, S // 2)
         scatter("vector", 1, 0, S)
-        scatter("scalar", 0, S // 2, S)
-        store(0)
-        store(1)
         bound(3)
-        for t in range(2):
-            for c in range(chunks):
-                nc.gpsimd.tensor_scalar(pairs[c][:, 0, :, t], cols(t, c), 1.0, -0.0, MULT, ADD)
+        bound(4)
+        bound(5)
+        scatter("scalar", 0, S // 2, S)
+        store(1)
+        store(0)
+        for t in (1, 0):
+            for c in range(len(spans)):
+                place(t, c)
         scatter("vector", 2, 0, S)
-        scatter("scalar", 3, 0, S // 2)
-        scatter("scalar", 3, S // 2, S)
+        scatter("scalar", 3, 0, 384)
         store(2)
+        scatter("vector", 3, 384, S)
         store(3)
-
-        on_vector = chunks // 2
-        for c in range(chunks):
-            if c < on_vector:
-                nc.vector.tensor_copy(pairs[c][:, 1, :, 0], cols(2, c))
-            else:
-                nc.vector.tensor_copy(pairs[c][:, 1], cols(2, c).unsqueeze(2).to_broadcast([P, CHUNK, 2]))
-        woven = [sb("woven%d" % c, [P, CHUNK, 2], F32) for c in range(chunks)]
-        for c in range(chunks):
-            if c < on_vector:
-                nc.vector.tensor_copy(pairs[c][:, 1, :, 1], cols(3, c))
-            else:
-                nc.scalar.copy(pairs[c][:, 1, :, 1], cols(3, c))
-                nc.scalar.copy(woven[c][:], pairs[c][:].rearrange("p u c e -> p (u c e)").bitcast(F32).rearrange("p (u c) -> p c u", u=2))
-        for c in range(on_vector):
-            nc.vector.tensor_copy(woven[c][:], pairs[c][:].rearrange("p u c e -> p (u c e)").bitcast(F32).rearrange("p (u c) -> p c u", u=2))
+        for t in (2, 3):
+            for c in range(len(spans)):
+                place(t, c)
+        for c in range(len(spans)):
+            weave(c)
         codes = sb("codes", [P, U], U32)
         plane = sb("plane", [P, U], U8)
         out_words = out_1[0].rearrange("p c r -> p (c r)").bitcast(I32)
-        for c in range(chunks):
-            lo, hi = c * CHUNK, (c + 1) * CHUNK
+        for c, (lo, hi, engine) in enumerate(spans):
             nc.vector.quantize_mx(out=codes[:, lo:hi].bitcast(FP8X4), scales=plane[:, lo:hi], in_=woven[c][:].rearrange("p c u -> p (c u)").bitcast(BF16))
             nc.sync.dma_start(out_words[:, lo:hi], codes[:, lo:hi].bitcast(I32))
         for q in range(4):

@@ -21,9 +21,7 @@ P = 128
 PACK = 4
 PASSES = 2
 LIST_ROWS = 16
-HALF = N // 2
-WORDS = P // 2
-ON_VECTOR = 40
+ON_VECTOR = 84
 
 
 def tile_picked_zkvw_tanh_po_kernel(tc, x_words, x_scales, cache, w1, scale, offs, slot, out_0, out_1, out_2):
@@ -39,7 +37,7 @@ def tile_picked_zkvw_tanh_po_kernel(tc, x_words, x_scales, cache, w1, scale, off
         slot_sb = sb("slot_sb", [P, S // LIST_ROWS], U16)
         xw = [sb("xw%d" % g, [P, T], U32) for g in range(PASSES)]
         xs = sb("xs", [P, T], U8)
-        w_raw = [[sb("w_raw%d_%d" % (g, h), [P, PACK, HALF], F32) for h in range(2)] for g in range(PASSES)]
+        w_raw = [[sb("w_raw%d_%d" % (g, h), [P, 2, N], F32) for h in range(2)] for g in range(PASSES)]
         scale_sb = sb("scale_sb", [P, S], F32)
         window = [sb("window%d" % t, [P, U], F32) for t in range(PACK)]
 
@@ -52,7 +50,7 @@ def tile_picked_zkvw_tanh_po_kernel(tc, x_words, x_scales, cache, w1, scale, off
 
         def load_w(g):
             for h in range(2):
-                nc.sync.dma_start(w_raw[g][h][:], w_rows[g][:, :, h * HALF : (h + 1) * HALF])
+                nc.sync.dma_start(w_raw[g][h][:], w_rows[g][:, 2 * h : 2 * h + 2, :])
 
         def plane_of(matrix, t):
             return matrix.rearrange("(l r) c -> l r c", r=PACK)[:, t, :]
@@ -79,7 +77,7 @@ def tile_picked_zkvw_tanh_po_kernel(tc, x_words, x_scales, cache, w1, scale, off
 
         def deal(g, h, engine, lo, hi):
             src = w_raw[g][h][:].rearrange("p j (l t) -> p l t j", t=PACK)[:, lo:hi]
-            dst = dealt[g][:].rearrange("p t l j -> p l t j")[:, h * WORDS + lo : h * WORDS + hi]
+            dst = dealt[g][:].rearrange("p t l j -> p l t j")[:, lo:hi, :, 2 * h : 2 * h + 2]
             if engine == "vector":
                 nc.vector.tensor_copy(dst, src)
             elif engine == "gpsimd":
@@ -95,15 +93,15 @@ def tile_picked_zkvw_tanh_po_kernel(tc, x_words, x_scales, cache, w1, scale, off
 
         nc.vector.tensor_copy(sg[:], xs[:].indirect(offs_sb[:]))
         nc.vector.tensor_copy(xg[0][:], xw[0][:].indirect(offs_sb[:]))
-        deal(0, 0, "scalar", 0, WORDS)
-        deal(0, 1, "scalar", 0, WORDS // 2)
-        deal(0, 1, "gpsimd", WORDS // 2, WORDS)
+        deal(0, 0, "scalar", 0, P)
+        deal(0, 1, "vector", 0, P)
         quantise_and_multiply(0)
         xg.append(sb("xg1", [P, S], U32, "dealt0"))
         nc.vector.tensor_copy(xg[1][:], xw[1][:].indirect(offs_sb[:]))
-        deal(1, 0, "scalar", 0, WORDS)
+        deal(1, 0, "scalar", 0, ON_VECTOR)
+        deal(1, 0, "gpsimd", ON_VECTOR, P)
         deal(1, 1, "vector", 0, ON_VECTOR)
-        deal(1, 1, "scalar", ON_VECTOR, WORDS)
+        deal(1, 1, "scalar", ON_VECTOR, P)
         quantise_and_multiply(1)
 
         scaled = [sb("scaled%d" % i, [P, hi - lo], F32) for i, (t, lo, hi) in enumerate(pieces)]

@@ -21,7 +21,7 @@ P = 128
 PACK = 4
 PASSES = 2
 LIST_ROWS = 16
-ON_VECTOR = 84
+ON_SCALAR = 52
 
 
 def tile_picked_zkvw_tanh_po_kernel(tc, x_words, x_scales, cache, w1, scale, offs, slot, out_0, out_1, out_2):
@@ -37,7 +37,8 @@ def tile_picked_zkvw_tanh_po_kernel(tc, x_words, x_scales, cache, w1, scale, off
         slot_sb = sb("slot_sb", [P, S // LIST_ROWS], U16)
         xw = [sb("xw%d" % g, [P, T], U32) for g in range(PASSES)]
         xs = sb("xs", [P, T], U8)
-        w_raw = [[sb("w_raw%d_%d" % (g, h), [P, 2, N], F32) for h in range(2)] for g in range(PASSES)]
+        parts = ((0, 0, 0, P), (0, 1, 0, P), (1, 0, 0, P), (1, 1, 0, ON_SCALAR), (1, 1, ON_SCALAR, P))
+        w_raw = [sb("w_raw%d" % i, [P, 2, PACK * (hi - lo)], F32) for i, (g, h, lo, hi) in enumerate(parts)]
         scale_sb = sb("scale_sb", [P, S], F32)
         window = [sb("window%d" % t, [P, U], F32) for t in range(PACK)]
 
@@ -48,9 +49,9 @@ def tile_picked_zkvw_tanh_po_kernel(tc, x_words, x_scales, cache, w1, scale, off
         def load_x(g):
             nc.sync.dma_start(xw[g][:].bitcast(I32), x_words[g].rearrange("p c r -> p (c r)").bitcast(I32))
 
-        def load_w(g):
-            for h in range(2):
-                nc.sync.dma_start(w_raw[g][h][:], w_rows[g][:, 2 * h : 2 * h + 2, :])
+        def load_w():
+            for i, (g, h, lo, hi) in enumerate(parts):
+                nc.sync.dma_start(w_raw[i][:], w_rows[g][:, 2 * h : 2 * h + 2, PACK * lo : PACK * hi])
 
         def plane_of(matrix, t):
             return matrix.rearrange("(l r) c -> l r c", r=PACK)[:, t, :]
@@ -59,15 +60,14 @@ def tile_picked_zkvw_tanh_po_kernel(tc, x_words, x_scales, cache, w1, scale, off
         nc.sync.dma_start(offs_sb[:], offs)
         for q in range(4):
             nc.sync.dma_start(xs[32 * q : 32 * q + 8, :].bitcast(I32), x_scales[:, 4 * q : 4 * q + 4, :].bitcast(I32))
-        load_w(0)
+        load_w()
         load_x(1)
-        load_w(1)
         nc.sync.dma_start(scale_sb[:], scale)
         nc.sync.dma_start(slot_sb[:], slot)
         for t, lo, hi in ((0, 0, U), (1, 0, U), (2, 0, 768), (3, 0, U), (2, 768, U)):
             nc.sync.dma_start(window[t][:, lo:hi], plane_of(cache, t)[:, lo:hi])
 
-        xg = [sb("xg0", [P, S], U32)]
+        xg = [sb("xg%d" % g, [P, S], U32) for g in range(PASSES)]
         sg = sb("sg", [P, S], U8)
         dealt = [sb("dealt%d" % g, [P, PACK, P, PACK], BF16) for g in range(PASSES)]
         w_q = [[sb("w_q%d_%d" % (g, t), [P, P], U32) for t in range(PACK)] for g in range(PASSES)]
@@ -75,9 +75,10 @@ def tile_picked_zkvw_tanh_po_kernel(tc, x_words, x_scales, cache, w1, scale, off
         pieces = ((1, 0, S // 2), (0, 0, S // 2), (1, S // 2, S), (0, S // 2, S), (2, 0, S), (3, 0, S))
         sums = [psum.tile([P, hi - lo], F32, name="sums%d" % i, tag="sums%d" % i) for i, (t, lo, hi) in enumerate(pieces)]
 
-        def deal(g, h, engine, lo, hi):
-            src = w_raw[g][h][:].rearrange("p j (l t) -> p l t j", t=PACK)[:, lo:hi]
-            dst = dealt[g][:].rearrange("p t l j -> p l t j")[:, lo:hi, :, 2 * h : 2 * h + 2]
+        def deal(i, engine, lo, hi, planes=slice(0, PACK)):
+            g, h, first, end = parts[i]
+            src = w_raw[i][:].rearrange("p j (l t) -> p l t j", t=PACK)[:, lo - first : hi - first, planes]
+            dst = dealt[g][:].rearrange("p t l j -> p l t j")[:, lo:hi, planes, 2 * h : 2 * h + 2]
             if engine == "vector":
                 nc.vector.tensor_copy(dst, src)
             elif engine == "gpsimd":
@@ -85,24 +86,30 @@ def tile_picked_zkvw_tanh_po_kernel(tc, x_words, x_scales, cache, w1, scale, off
             else:
                 nc.scalar.copy(dst, src)
 
-        def quantise_and_multiply(g):
+        def quantise(g):
             for t in (1, 0, 2, 3):
                 nc.vector.quantize_mx(out=w_q[g][t][:].bitcast(FP8X4), scales=w_s[g][t][:], in_=dealt[g][:, t].rearrange("p l j -> p (l j)"))
+
+        def multiply(g):
             for i, (t, lo, hi) in enumerate(pieces):
                 nc.tensor.matmul_mx(out=sums[i][:], lhsT=w_q[g][t][:].bitcast(FP8X4), lhsT_scale=w_s[g][t][:], rhs=xg[g][:, lo:hi].bitcast(FP8X4), rhs_scale=sg[4 * g : P, lo:hi], start=g == 0, stop=g == PASSES - 1)
 
         nc.vector.tensor_copy(sg[:], xs[:].indirect(offs_sb[:]))
         nc.vector.tensor_copy(xg[0][:], xw[0][:].indirect(offs_sb[:]))
-        deal(0, 0, "scalar", 0, P)
-        deal(0, 1, "vector", 0, P)
-        quantise_and_multiply(0)
-        xg.append(sb("xg1", [P, S], U32, "dealt0"))
-        nc.vector.tensor_copy(xg[1][:], xw[1][:].indirect(offs_sb[:]))
-        deal(1, 0, "scalar", 0, ON_VECTOR)
-        deal(1, 0, "gpsimd", ON_VECTOR, P)
-        deal(1, 1, "vector", 0, ON_VECTOR)
-        deal(1, 1, "scalar", ON_VECTOR, P)
-        quantise_and_multiply(1)
+        for h in range(2):
+            deal(h, "scalar", 0, 64)
+            deal(h, "gpsimd", 64, P)
+        quantise(0)
+        multiply(0)
+        deal(2, "scalar", 0, ON_SCALAR)
+        deal(2, "vector", ON_SCALAR, P)
+        deal(3, "scalar", 0, ON_SCALAR)
+        deal(4, "vector", ON_SCALAR, P, slice(0, 2))
+        deal(4, "vector", ON_SCALAR, P, slice(2, PACK))
+        quantise(1)
+        for lo, hi in ((0, S // 2), (S // 2, S)):
+            nc.vector.tensor_copy(xg[1][:, lo:hi], xw[1][:].indirect(offs_sb[:, lo // LIST_ROWS : hi // LIST_ROWS]))
+        multiply(1)
 
         scaled = [sb("scaled%d" % i, [P, hi - lo], F32) for i, (t, lo, hi) in enumerate(pieces)]
         for i, (t, lo, hi) in enumerate(pieces):
@@ -111,14 +118,16 @@ def tile_picked_zkvw_tanh_po_kernel(tc, x_words, x_scales, cache, w1, scale, off
         early = sb("early", [P, S // 2], F32)
         whole = sb("whole", [P, S], F32)
         late = sb("late", [P, S // 2 + S], F32, "scale_sb")
-        last = sb("last", [P, S], F32)
+        last = [sb("last0", [P, 384], F32), sb("last1", [P, S - 384], F32)]
 
         def bounded(t, lo, hi):
             if t == 0:
                 return early[:, lo:hi] if hi <= S // 2 else late[:, lo - S // 2 : hi - S // 2]
             if t == 2:
                 return late[:, S // 2 + lo : S // 2 + hi]
-            return (whole if t == 1 else last)[:, lo:hi]
+            if t == 3:
+                return last[lo // 384][:]
+            return whole[:, lo:hi]
 
         def bound(i):
             nc.scalar.activation(bounded(*pieces[i]), scaled[i][:], TANH)
@@ -134,13 +143,13 @@ def tile_picked_zkvw_tanh_po_kernel(tc, x_words, x_scales, cache, w1, scale, off
             nc.sync.dma_start(plane_of(out_0, t), window[t][:])
 
         spans = ((0, 256, "vector"), (256, 512, "vector"), (512, 896, "scalar"), (896, 1024, "scalar"))
-        pairs = [sb("pairs%d" % c, [P, 2, hi - lo, 2], BF16) for c, (lo, hi, engine) in enumerate(spans)]
+        pairs = [sb("pairs%d" % c, [P, 2, hi - lo, 2], BF16) for c, (lo, hi, engine) in enumerate(spans[0:3])]
         woven = [sb("woven%d" % c, [P, hi - lo, 2], F32) for c, (lo, hi, engine) in enumerate(spans)]
 
         def place(t, c):
             lo, hi, engine = spans[c]
             dst, src = pairs[c][:, t // 2, :, t % 2], window[t][:, lo:hi]
-            if t < 2:
+            if t < 2 and c < 3:
                 nc.gpsimd.tensor_scalar(dst, src, 1.0, -0.0, MULT, ADD)
             elif engine == "vector":
                 nc.vector.tensor_copy(dst, src)
@@ -161,15 +170,19 @@ def tile_picked_zkvw_tanh_po_kernel(tc, x_words, x_scales, cache, w1, scale, off
         scatter("vector", 1, 0, S)
         bound(3)
         bound(4)
-        bound(5)
+        nc.scalar.activation(last[0][:], scaled[5][:, 0:384], TANH)
+        nc.scalar.activation(last[1][:], scaled[5][:, 384:S], TANH)
         scatter("scalar", 0, S // 2, S)
         store(1)
         store(0)
         for t in (1, 0):
-            for c in range(len(spans)):
+            for c in range(3):
                 place(t, c)
         scatter("vector", 2, 0, S)
         scatter("scalar", 3, 0, 384)
+        pairs.append(sb("pairs3", [P, 2, 128, 2], BF16, "last0"))
+        place(0, 3)
+        place(1, 3)
         store(2)
         scatter("vector", 3, 384, S)
         store(3)

@@ -37,12 +37,12 @@ def tile_picked_zkvw_tanh_po_kernel(tc, x_words, x_scales, cache, w1, scale, off
         slot_sb = sb("slot_sb", [P, S // LIST_ROWS], U16)
         xw = [sb("xw%d" % g, [P, T], U32) for g in range(PASSES)]
         xs = sb("xs", [P, T], U8)
-        parts = ((0, 0, 0, P), (0, 1, 0, P), (1, 0, 0, P), (1, 1, 0, ON_SCALAR), (1, 1, ON_SCALAR, P))
-        w_raw = [sb("w_raw%d" % i, [P, 2, PACK * (hi - lo)], F32) for i, (g, h, lo, hi) in enumerate(parts)]
+        parts = ((0, slice(0, 4), 0, P), (1, slice(0, 2), 0, P), (1, slice(2, 4), 0, ON_SCALAR), (1, slice(2, 4), ON_SCALAR, P))
+        w_raw = [sb("w_raw%d" % i, [P, rows.stop - rows.start, PACK * (hi - lo)], F32) for i, (g, rows, lo, hi) in enumerate(parts)]
         scale_sb = sb("scale_sb", [P, S], F32)
         window = [sb("window%d" % t, [P, U], F32) for t in range(PACK)]
 
-        nc.gpsimd.memset(xs[:].bitcast(I32), 0)
+        nc.vector.memset(xs[:].bitcast(I32), 0)
 
         w_rows = w1.rearrange("(g p j) n -> g p j n", g=PASSES, j=PACK)
 
@@ -50,8 +50,8 @@ def tile_picked_zkvw_tanh_po_kernel(tc, x_words, x_scales, cache, w1, scale, off
             nc.sync.dma_start(xw[g][:].bitcast(I32), x_words[g].rearrange("p c r -> p (c r)").bitcast(I32))
 
         def load_w():
-            for i, (g, h, lo, hi) in enumerate(parts):
-                nc.sync.dma_start(w_raw[i][:], w_rows[g][:, 2 * h : 2 * h + 2, PACK * lo : PACK * hi])
+            for i, (g, rows, lo, hi) in enumerate(parts):
+                nc.sync.dma_start(w_raw[i][:], w_rows[g][:, rows, PACK * lo : PACK * hi])
 
         def plane_of(matrix, t):
             return matrix.rearrange("(l r) c -> l r c", r=PACK)[:, t, :]
@@ -76,13 +76,11 @@ def tile_picked_zkvw_tanh_po_kernel(tc, x_words, x_scales, cache, w1, scale, off
         sums = [psum.tile([P, hi - lo], F32, name="sums%d" % i, tag="sums%d" % i) for i, (t, lo, hi) in enumerate(pieces)]
 
         def deal(i, engine, lo, hi, planes=slice(0, PACK)):
-            g, h, first, end = parts[i]
+            g, rows, first, end = parts[i]
             src = w_raw[i][:].rearrange("p j (l t) -> p l t j", t=PACK)[:, lo - first : hi - first, planes]
-            dst = dealt[g][:].rearrange("p t l j -> p l t j")[:, lo:hi, planes, 2 * h : 2 * h + 2]
+            dst = dealt[g][:].rearrange("p t l j -> p l t j")[:, lo:hi, planes, rows]
             if engine == "vector":
                 nc.vector.tensor_copy(dst, src)
-            elif engine == "gpsimd":
-                nc.gpsimd.tensor_scalar(dst, src, 1.0, -0.0, MULT, ADD)
             else:
                 nc.scalar.copy(dst, src)
 
@@ -96,16 +94,15 @@ def tile_picked_zkvw_tanh_po_kernel(tc, x_words, x_scales, cache, w1, scale, off
 
         nc.vector.tensor_copy(sg[:], xs[:].indirect(offs_sb[:]))
         nc.vector.tensor_copy(xg[0][:], xw[0][:].indirect(offs_sb[:]))
-        for h in range(2):
-            deal(h, "scalar", 0, 64)
-            deal(h, "gpsimd", 64, P)
+        deal(0, "scalar", 0, 40)
+        deal(0, "vector", 40, P)
         quantise(0)
         multiply(0)
+        deal(1, "scalar", 0, ON_SCALAR)
+        deal(1, "vector", ON_SCALAR, P)
         deal(2, "scalar", 0, ON_SCALAR)
-        deal(2, "vector", ON_SCALAR, P)
-        deal(3, "scalar", 0, ON_SCALAR)
-        deal(4, "vector", ON_SCALAR, P, slice(0, 2))
-        deal(4, "vector", ON_SCALAR, P, slice(2, PACK))
+        deal(3, "vector", ON_SCALAR, P, slice(0, 2))
+        deal(3, "vector", ON_SCALAR, P, slice(2, PACK))
         quantise(1)
         for lo, hi in ((0, S // 2), (S // 2, S)):
             nc.vector.tensor_copy(xg[1][:, lo:hi], xw[1][:].indirect(offs_sb[:, lo // LIST_ROWS : hi // LIST_ROWS]))
@@ -118,7 +115,7 @@ def tile_picked_zkvw_tanh_po_kernel(tc, x_words, x_scales, cache, w1, scale, off
         early = sb("early", [P, S // 2], F32)
         whole = sb("whole", [P, S], F32)
         late = sb("late", [P, S // 2 + S], F32, "scale_sb")
-        last = [sb("last0", [P, 384], F32), sb("last1", [P, S - 384], F32)]
+        last = sb("last", [P, S], F32)
 
         def bounded(t, lo, hi):
             if t == 0:
@@ -126,7 +123,7 @@ def tile_picked_zkvw_tanh_po_kernel(tc, x_words, x_scales, cache, w1, scale, off
             if t == 2:
                 return late[:, S // 2 + lo : S // 2 + hi]
             if t == 3:
-                return last[lo // 384][:]
+                return last[:, lo:hi]
             return whole[:, lo:hi]
 
         def bound(i):
@@ -143,7 +140,8 @@ def tile_picked_zkvw_tanh_po_kernel(tc, x_words, x_scales, cache, w1, scale, off
             nc.sync.dma_start(plane_of(out_0, t), window[t][:])
 
         spans = ((0, 256, "vector"), (256, 512, "vector"), (512, 896, "scalar"), (896, 1024, "scalar"))
-        pairs = [sb("pairs%d" % c, [P, 2, hi - lo, 2], BF16) for c, (lo, hi, engine) in enumerate(spans[0:3])]
+        pairs = [sb("pairs%d" % c, [P, 2, hi - lo, 2], BF16)[:] for c, (lo, hi, engine) in enumerate(spans[0:3])]
+        pairs.append(last[:, 0:256].bitcast(BF16).rearrange("p (u c e) -> p u c e", u=2, e=2))
         woven = [sb("woven%d" % c, [P, hi - lo, 2], F32) for c, (lo, hi, engine) in enumerate(spans)]
 
         def place(t, c):
@@ -157,7 +155,7 @@ def tile_picked_zkvw_tanh_po_kernel(tc, x_words, x_scales, cache, w1, scale, off
                 nc.scalar.copy(dst, src)
 
         def weave(c):
-            src = pairs[c][:].rearrange("p u c e -> p (u c e)").bitcast(F32).rearrange("p (u c) -> p c u", u=2)
+            src = pairs[c].rearrange("p u c e -> p (u c e)").bitcast(F32).rearrange("p (u c) -> p c u", u=2)
             if spans[c][2] == "vector":
                 nc.vector.tensor_copy(woven[c][:], src)
             else:
@@ -170,8 +168,7 @@ def tile_picked_zkvw_tanh_po_kernel(tc, x_words, x_scales, cache, w1, scale, off
         scatter("vector", 1, 0, S)
         bound(3)
         bound(4)
-        nc.scalar.activation(last[0][:], scaled[5][:, 0:384], TANH)
-        nc.scalar.activation(last[1][:], scaled[5][:, 384:S], TANH)
+        bound(5)
         scatter("scalar", 0, S // 2, S)
         store(1)
         store(0)
@@ -180,7 +177,6 @@ def tile_picked_zkvw_tanh_po_kernel(tc, x_words, x_scales, cache, w1, scale, off
                 place(t, c)
         scatter("vector", 2, 0, S)
         scatter("scalar", 3, 0, 384)
-        pairs.append(sb("pairs3", [P, 2, 128, 2], BF16, "last0"))
         place(0, 3)
         place(1, 3)
         store(2)

@@ -108,26 +108,24 @@ def tile_picked_zkvw_tanh_po_kernel(tc, x_words, x_scales, cache, w1, scale, off
             nc.vector.tensor_copy(xg[1][:, lo:hi], xw[1][:].indirect(offs_sb[:, lo // LIST_ROWS : hi // LIST_ROWS]))
         multiply(1)
 
-        scaled = [sb("scaled%d" % i, [P, hi - lo], F32) for i, (t, lo, hi) in enumerate(pieces)]
+        first = 3
+        starts = [sum(hi - lo for t, lo, hi in pieces[first:i]) for i in range(first, len(pieces) + 1)]
+        scaled_late = sb("scaled_late", [P, starts[-1]], F32)
+        scaled = [sb("scaled%d" % i, [P, S // 2], F32)[:] for i in range(first)]
+        scaled += [scaled_late[:, lo:hi] for lo, hi in zip(starts, starts[1:])]
         for i, (t, lo, hi) in enumerate(pieces):
-            nc.vector.tensor_tensor(scaled[i][:], sums[i][:], scale_sb[:, lo:hi], MULT)
+            nc.vector.tensor_tensor(scaled[i], sums[i][:], scale_sb[:, lo:hi], MULT)
 
         early = sb("early", [P, S // 2], F32)
         whole = sb("whole", [P, S], F32)
-        late = sb("late", [P, S // 2 + S], F32, "scale_sb")
-        last = sb("last", [P, S], F32)
+        late = sb("late", [P, starts[-1]], F32, "scale_sb")
 
         def bounded(t, lo, hi):
+            if t == 1:
+                return whole[:, lo:hi]
             if t == 0:
                 return early[:, lo:hi] if hi <= S // 2 else late[:, lo - S // 2 : hi - S // 2]
-            if t == 2:
-                return late[:, S // 2 + lo : S // 2 + hi]
-            if t == 3:
-                return last[:, lo:hi]
-            return whole[:, lo:hi]
-
-        def bound(i):
-            nc.scalar.activation(bounded(*pieces[i]), scaled[i][:], TANH)
+            return late[:, starts[t - 1] + lo : starts[t - 1] + hi]
 
         def scatter(engine, t, lo, hi):
             target = window[t][:].indirect(slot_sb[:, lo // LIST_ROWS : hi // LIST_ROWS])
@@ -140,51 +138,45 @@ def tile_picked_zkvw_tanh_po_kernel(tc, x_words, x_scales, cache, w1, scale, off
             nc.sync.dma_start(plane_of(out_0, t), window[t][:])
 
         spans = ((0, 256, "vector"), (256, 512, "vector"), (512, 896, "scalar"), (896, 1024, "scalar"))
-        pairs = [sb("pairs%d" % c, [P, 2, hi - lo, 2], BF16)[:] for c, (lo, hi, engine) in enumerate(spans[0:3])]
-        pairs.append(last[:, 0:256].bitcast(BF16).rearrange("p (u c e) -> p u c e", u=2, e=2))
+        joined = sb("joined", [P, 2, U, 2], BF16)
+        pairs = [joined[:, :, lo:hi] for lo, hi, engine in spans]
         woven = [sb("woven%d" % c, [P, hi - lo, 2], F32) for c, (lo, hi, engine) in enumerate(spans)]
 
         def place(t, c):
             lo, hi, engine = spans[c]
             dst, src = pairs[c][:, t // 2, :, t % 2], window[t][:, lo:hi]
-            if t < 2 and c < 3:
-                nc.gpsimd.tensor_scalar(dst, src, 1.0, -0.0, MULT, ADD)
-            elif engine == "vector":
+            if engine == "vector":
                 nc.vector.tensor_copy(dst, src)
             else:
                 nc.scalar.copy(dst, src)
 
         def weave(c):
-            src = pairs[c].rearrange("p u c e -> p (u c e)").bitcast(F32).rearrange("p (u c) -> p c u", u=2)
+            src = pairs[c].rearrange("p u c e -> p u (c e)").bitcast(F32).rearrange("p u c -> p c u")
             if spans[c][2] == "vector":
                 nc.vector.tensor_copy(woven[c][:], src)
             else:
                 nc.scalar.copy(woven[c][:], src)
 
-        bound(0)
-        bound(1)
-        bound(2)
+        for i in range(first):
+            nc.scalar.activation(bounded(*pieces[i]), scaled[i], TANH)
         scatter("scalar", 0, 0, S // 2)
         scatter("vector", 1, 0, S)
-        bound(3)
-        bound(4)
-        bound(5)
+        nc.scalar.activation(late[:, 0 : starts[1]], scaled_late[:, 0 : starts[1]], TANH)
+        nc.scalar.activation(late[:, starts[1] :], scaled_late[:, starts[1] :], TANH)
         scatter("scalar", 0, S // 2, S)
         store(1)
         store(0)
         for t in (1, 0):
-            for c in range(3):
-                place(t, c)
+            nc.gpsimd.tensor_scalar(joined[:, 0, :, t], window[t][:], 1.0, -0.0, MULT, ADD)
         scatter("vector", 2, 0, S)
         scatter("scalar", 3, 0, 384)
-        place(0, 3)
-        place(1, 3)
         store(2)
         scatter("vector", 3, 384, S)
         store(3)
-        for t in (2, 3):
-            for c in range(len(spans)):
-                place(t, c)
+        nc.vector.tensor_copy(joined[:, 1, 0:S, 0], window[2][:, 0:S])
+        nc.scalar.copy(joined[:, 1, S:U, 0], window[2][:, S:U])
+        for c in range(len(spans)):
+            place(3, c)
         for c in range(len(spans)):
             weave(c)
         codes = sb("codes", [P, U], U32)

@@ -137,7 +137,7 @@ def tile_picked_zkvw_tanh_po_kernel(tc, x_words, x_scales, cache, w1, scale, off
         def store(t):
             nc.sync.dma_start(plane_of(out_0, t), window[t][:])
 
-        spans = ((0, 256, "vector"), (256, 512, "vector"), (512, 896, "scalar"), (896, 1024, "scalar"))
+        spans = ((0, 256, "vector"), (256, 512, "vector"), (512, 768, "scalar"), (768, 896, "scalar"), (896, 1024, "scalar"))
         joined = sb("joined", [P, 2, U, 2], BF16)
         pairs = [joined[:, :, lo:hi] for lo, hi, engine in spans]
         woven = [sb("woven%d" % c, [P, hi - lo, 2], F32) for c, (lo, hi, engine) in enumerate(spans)]
@@ -173,18 +173,31 @@ def tile_picked_zkvw_tanh_po_kernel(tc, x_words, x_scales, cache, w1, scale, off
         store(2)
         scatter("vector", 3, 384, S)
         store(3)
-        nc.vector.tensor_copy(joined[:, 1, 0:S, 0], window[2][:, 0:S])
-        nc.scalar.copy(joined[:, 1, S:U, 0], window[2][:, S:U])
-        for c in range(len(spans)):
-            place(3, c)
-        for c in range(len(spans)):
-            weave(c)
         codes = sb("codes", [P, U], U32)
         plane = sb("plane", [P, U], U8)
         out_words = out_1[0].rearrange("p c r -> p (c r)").bitcast(I32)
-        for c, (lo, hi, engine) in enumerate(spans):
+
+        def quantise_span(c):
+            lo, hi, engine = spans[c]
             nc.vector.quantize_mx(out=codes[:, lo:hi].bitcast(FP8X4), scales=plane[:, lo:hi], in_=woven[c][:].rearrange("p c u -> p (c u)").bitcast(BF16))
-            nc.sync.dma_start(out_words[:, lo:hi], codes[:, lo:hi].bitcast(I32))
+            if c != 3:
+                since = spans[3][0] if c == 4 else lo
+                nc.sync.dma_start(out_words[:, since:hi], codes[:, since:hi].bitcast(I32))
+
+        nc.scalar.copy(joined[:, 1, S:U, 0], window[2][:, S:U])
+        place(3, 2)
+        nc.scalar.copy(joined[:, 1, 768:U, 1], window[3][:, 768:U])
+        for c in range(2, len(spans)):
+            weave(c)
+        place(2, 0)
+        place(3, 0)
+        place(2, 1)
+        weave(0)
+        place(3, 1)
+        quantise_span(0)
+        weave(1)
+        for c in (2, 1, 3, 4):
+            quantise_span(c)
         for q in range(4):
             queue = nc.sync if q == 0 else nc.scalar
             queue.dma_start(out_2[0, 4 * q : 4 * q + 4, :].bitcast(I32), plane[32 * q : 32 * q + 4, :].bitcast(I32))

@@ -84,6 +84,14 @@ def tile_picked_zkvw_tanh_po_kernel(tc, x_words, x_scales, cache, w1, scale, off
             else:
                 nc.scalar.copy(dst, src)
 
+        def deal_rows(i, engine, lo, hi):
+            src = w_raw[i][:].rearrange("p j (l u e) -> p u l e j", u=2, e=2)[:, :, lo:hi]
+            dst = dealt[parts[i][0]][:].rearrange("p (u e) l j -> p u l e j", e=2)[:, :, lo:hi]
+            if engine == "vector":
+                nc.vector.tensor_copy(dst, src)
+            else:
+                nc.scalar.copy(dst, src)
+
         def quantise(g):
             for t in (1, 0, 2, 3):
                 nc.vector.quantize_mx(out=w_q[g][t][:].bitcast(FP8X4), scales=w_s[g][t][:], in_=dealt[g][:, t].rearrange("p l j -> p (l j)"))
@@ -94,8 +102,8 @@ def tile_picked_zkvw_tanh_po_kernel(tc, x_words, x_scales, cache, w1, scale, off
 
         nc.vector.tensor_copy(sg[:], xs[:].indirect(offs_sb[:]))
         nc.vector.tensor_copy(xg[0][:], xw[0][:].indirect(offs_sb[:]))
-        deal(0, "scalar", 0, 40)
-        deal(0, "vector", 40, P)
+        deal_rows(0, "scalar", 0, 40)
+        deal_rows(0, "vector", 40, P)
         quantise(0)
         multiply(0)
         deal(1, "scalar", 0, ON_SCALAR)

@@ -21,7 +21,8 @@ P = 128
 PACK = 4
 PASSES = 2
 LIST_ROWS = 16
-ON_SCALAR = 52
+ON_SCALAR = 64
+FIRST_PAIR_ON_SCALAR = 52
 
 
 def tile_picked_zkvw_tanh_po_kernel(tc, x_words, x_scales, cache, w1, scale, offs, slot, out_0, out_1, out_2):
@@ -72,7 +73,7 @@ def tile_picked_zkvw_tanh_po_kernel(tc, x_words, x_scales, cache, w1, scale, off
         dealt = [sb("dealt%d" % g, [P, PACK, P, PACK], BF16) for g in range(PASSES)]
         w_q = [[sb("w_q%d_%d" % (g, t), [P, P], U32) for t in range(PACK)] for g in range(PASSES)]
         w_s = [[sb("w_s%d_%d" % (g, t), [P, P], U8) for t in range(PACK)] for g in range(PASSES)]
-        pieces = ((1, 0, S // 2), (0, 0, S // 2), (1, S // 2, S), (0, S // 2, S), (2, 0, S), (3, 0, S))
+        pieces = ((1, 0, S // 2), (0, 0, S // 2), (1, S // 2, S), (0, S // 2, S), (2, 0, S), (3, 0, S // 2), (3, S // 2, S))
         sums = [psum.tile([P, hi - lo], F32, name="sums%d" % i, tag="sums%d" % i) for i, (t, lo, hi) in enumerate(pieces)]
 
         def deal(i, engine, lo, hi, planes=slice(0, PACK)):
@@ -97,17 +98,18 @@ def tile_picked_zkvw_tanh_po_kernel(tc, x_words, x_scales, cache, w1, scale, off
                 nc.vector.quantize_mx(out=w_q[g][t][:].bitcast(FP8X4), scales=w_s[g][t][:], in_=dealt[g][:, t].rearrange("p l j -> p (l j)"))
 
         def multiply(g):
-            for i, (t, lo, hi) in enumerate(pieces):
+            for i in (0, 5, 1, 2, 3, 4, 6):
+                t, lo, hi = pieces[i]
                 nc.tensor.matmul_mx(out=sums[i][:], lhsT=w_q[g][t][:].bitcast(FP8X4), lhsT_scale=w_s[g][t][:], rhs=xg[g][:, lo:hi].bitcast(FP8X4), rhs_scale=sg[4 * g : P, lo:hi], start=g == 0, stop=g == PASSES - 1)
 
         nc.vector.tensor_copy(sg[:], xs[:].indirect(offs_sb[:]))
         nc.vector.tensor_copy(xg[0][:], xw[0][:].indirect(offs_sb[:]))
-        deal_rows(0, "scalar", 0, 40)
-        deal_rows(0, "vector", 40, P)
+        deal_rows(0, "scalar", 0, 32)
+        deal_rows(0, "vector", 32, P)
         quantise(0)
         multiply(0)
-        deal(1, "scalar", 0, ON_SCALAR)
-        deal(1, "vector", ON_SCALAR, P)
+        deal(1, "scalar", 0, FIRST_PAIR_ON_SCALAR)
+        deal(1, "vector", FIRST_PAIR_ON_SCALAR, P)
         deal(2, "scalar", 0, ON_SCALAR)
         deal(3, "vector", ON_SCALAR, P, slice(0, 2))
         deal(3, "vector", ON_SCALAR, P, slice(2, PACK))
@@ -121,8 +123,13 @@ def tile_picked_zkvw_tanh_po_kernel(tc, x_words, x_scales, cache, w1, scale, off
         scaled_late = sb("scaled_late", [P, starts[-1]], F32)
         scaled = [sb("scaled%d" % i, [P, S // 2], F32)[:] for i in range(first)]
         scaled += [scaled_late[:, lo:hi] for lo, hi in zip(starts, starts[1:])]
+        moved = sb("moved", [P, S // 2], F32)
+        nc.scalar.copy(moved[:], sums[5][:])
         for i, (t, lo, hi) in enumerate(pieces):
-            nc.vector.tensor_tensor(scaled[i], sums[i][:], scale_sb[:, lo:hi], MULT)
+            if i == 5:
+                nc.gpsimd.tensor_tensor(scaled[i], moved[:], scale_sb[:, lo:hi], MULT)
+            else:
+                nc.vector.tensor_tensor(scaled[i], sums[i][:], scale_sb[:, lo:hi], MULT)
 
         early = sb("early", [P, S // 2], F32)
         whole = sb("whole", [P, S], F32)
@@ -176,11 +183,11 @@ def tile_picked_zkvw_tanh_po_kernel(tc, x_words, x_scales, cache, w1, scale, off
         store(0)
         for t in (1, 0):
             nc.gpsimd.tensor_scalar(joined[:, 0, :, t], window[t][:], 1.0, -0.0, MULT, ADD)
+        scatter("vector", 3, 0, 128)
         scatter("vector", 2, 0, S)
-        scatter("scalar", 3, 0, 384)
-        store(2)
-        scatter("vector", 3, 384, S)
+        scatter("scalar", 3, 128, S)
         store(3)
+        store(2)
         codes = sb("codes", [P, U], U32)
         plane = sb("plane", [P, U], U8)
         out_words = out_1[0].rearrange("p c r -> p (c r)").bitcast(I32)
@@ -192,16 +199,16 @@ def tile_picked_zkvw_tanh_po_kernel(tc, x_words, x_scales, cache, w1, scale, off
                 since = spans[3][0] if c == 4 else lo
                 nc.sync.dma_start(out_words[:, since:hi], codes[:, since:hi].bitcast(I32))
 
-        nc.scalar.copy(joined[:, 1, S:U, 0], window[2][:, S:U])
-        place(3, 2)
-        nc.scalar.copy(joined[:, 1, 768:U, 1], window[3][:, 768:U])
+        nc.scalar.copy(joined[:, 1, S:U, 1], window[3][:, S:U])
+        place(2, 2)
+        nc.scalar.copy(joined[:, 1, 768:U, 0], window[2][:, 768:U])
         for c in range(2, len(spans)):
             weave(c)
-        place(2, 0)
         place(3, 0)
+        place(3, 1)
+        place(2, 0)
         place(2, 1)
         weave(0)
-        place(3, 1)
         quantise_span(0)
         weave(1)
         for c in (2, 1, 3, 4):

@@ -21,6 +21,7 @@ P = 128
 PACK = 4
 PASSES = 2
 LIST_ROWS = 16
+BORDER = 512
 ON_SCALAR = 64
 FIRST_PAIR_ON_SCALAR = 52
 
@@ -152,18 +153,10 @@ def tile_picked_zkvw_tanh_po_kernel(tc, x_words, x_scales, cache, w1, scale, off
         def store(t):
             nc.sync.dma_start(plane_of(out_0, t), window[t][:])
 
-        spans = ((0, 256, "vector"), (256, 512, "vector"), (512, 768, "scalar"), (768, 896, "scalar"), (896, 1024, "scalar"))
+        spans = ((0, 256, "vector"), (256, 512, "vector"), (512, 640, "scalar"), (640, 896, "scalar"), (896, 1024, "scalar"))
         joined = sb("joined", [P, 2, U, 2], BF16)
         pairs = [joined[:, :, lo:hi] for lo, hi, engine in spans]
         woven = [sb("woven%d" % c, [P, hi - lo, 2], F32) for c, (lo, hi, engine) in enumerate(spans)]
-
-        def place(t, c):
-            lo, hi, engine = spans[c]
-            dst, src = pairs[c][:, t // 2, :, t % 2], window[t][:, lo:hi]
-            if engine == "vector":
-                nc.vector.tensor_copy(dst, src)
-            else:
-                nc.scalar.copy(dst, src)
 
         def weave(c):
             src = pairs[c].rearrange("p u c e -> p u (c e)").bitcast(F32).rearrange("p u c -> p c u")
@@ -195,20 +188,30 @@ def tile_picked_zkvw_tanh_po_kernel(tc, x_words, x_scales, cache, w1, scale, off
         def quantise_span(c):
             lo, hi, engine = spans[c]
             nc.vector.quantize_mx(out=codes[:, lo:hi].bitcast(FP8X4), scales=plane[:, lo:hi], in_=woven[c][:].rearrange("p c u -> p (c u)").bitcast(BF16))
-            if c != 3:
-                since = spans[3][0] if c == 4 else lo
+            if c != 2:
+                since = lo
+                hi = spans[2][1] if c == 1 else hi
                 nc.sync.dma_start(out_words[:, since:hi], codes[:, since:hi].bitcast(I32))
 
-        nc.scalar.copy(joined[:, 1, S:U, 1], window[3][:, S:U])
-        place(2, 2)
-        nc.scalar.copy(joined[:, 1, 768:U, 0], window[2][:, 768:U])
-        for c in range(2, len(spans)):
-            weave(c)
-        place(3, 0)
-        place(3, 1)
-        place(2, 0)
-        place(2, 1)
+        def put(engine, t, lo, hi):
+            dst, src = joined[:, 1, lo:hi, t % 2], window[t][:, lo:hi]
+            if engine == "vector":
+                nc.vector.tensor_copy(dst, src)
+            else:
+                nc.scalar.copy(dst, src)
+
+        put("scalar", 3, BORDER, U)
+        put("scalar", 2, *spans[2][:2])
+        put("scalar", 2, *spans[3][:2])
+        weave(2)
+        put("scalar", 2, *spans[4][:2])
+        weave(3)
+        weave(4)
+        put("vector", 3, *spans[0][:2])
+        put("vector", 2, *spans[0][:2])
+        put("vector", 3, *spans[1][:2])
         weave(0)
+        put("vector", 2, *spans[1][:2])
         quantise_span(0)
         weave(1)
         for c in (2, 1, 3, 4):

@@ -22,8 +22,8 @@ PACK = 4
 PASSES = 2
 LIST_ROWS = 16
 BORDER = 512
-ON_SCALAR = 64
-FIRST_PAIR_ON_SCALAR = 52
+ON_SCALAR = 56
+FIRST_PAIR_ON_SCALAR = 64
 
 
 def tile_picked_zkvw_tanh_po_kernel(tc, x_words, x_scales, cache, w1, scale, offs, slot, out_0, out_1, out_2):
@@ -39,7 +39,7 @@ def tile_picked_zkvw_tanh_po_kernel(tc, x_words, x_scales, cache, w1, scale, off
         slot_sb = sb("slot_sb", [P, S // LIST_ROWS], U16)
         xw = [sb("xw%d" % g, [P, T], U32) for g in range(PASSES)]
         xs = sb("xs", [P, T], U8)
-        parts = ((0, slice(0, 4), 0, P), (1, slice(0, 2), 0, P), (1, slice(2, 4), 0, ON_SCALAR), (1, slice(2, 4), ON_SCALAR, P))
+        parts = ((0, slice(0, 4), 0, P), (1, slice(0, 2), 0, P), (1, slice(2, 4), 0, P))
         w_raw = [sb("w_raw%d" % i, [P, rows.stop - rows.start, PACK * (hi - lo)], F32) for i, (g, rows, lo, hi) in enumerate(parts)]
         scale_sb = sb("scale_sb", [P, S], F32)
         window = [sb("window%d" % t, [P, U], F32) for t in range(PACK)]
@@ -66,7 +66,7 @@ def tile_picked_zkvw_tanh_po_kernel(tc, x_words, x_scales, cache, w1, scale, off
         load_x(1)
         nc.sync.dma_start(scale_sb[:], scale)
         nc.sync.dma_start(slot_sb[:], slot)
-        for t, lo, hi in ((0, 0, U), (1, 0, U), (2, 0, 768), (3, 0, U), (2, 768, U)):
+        for t, lo, hi in ((0, 0, U), (1, 0, U), (2, 0, 768), (3, 0, S), (3, S, U), (2, 768, U)):
             nc.sync.dma_start(window[t][:, lo:hi], plane_of(cache, t)[:, lo:hi])
 
         xg = [sb("xg%d" % g, [P, S], U32) for g in range(PASSES)]
@@ -77,18 +77,10 @@ def tile_picked_zkvw_tanh_po_kernel(tc, x_words, x_scales, cache, w1, scale, off
         pieces = ((1, 0, S // 2), (0, 0, S // 2), (1, S // 2, S), (0, S // 2, S), (2, 0, S), (3, 0, S // 2), (3, S // 2, S))
         sums = [psum.tile([P, hi - lo], F32, name="sums%d" % i, tag="sums%d" % i) for i, (t, lo, hi) in enumerate(pieces)]
 
-        def deal(i, engine, lo, hi, planes=slice(0, PACK)):
+        def deal(i, engine, lo, hi, halves=slice(0, 2)):
             g, rows, first, end = parts[i]
-            src = w_raw[i][:].rearrange("p j (l t) -> p l t j", t=PACK)[:, lo - first : hi - first, planes]
-            dst = dealt[g][:].rearrange("p t l j -> p l t j")[:, lo:hi, planes, rows]
-            if engine == "vector":
-                nc.vector.tensor_copy(dst, src)
-            else:
-                nc.scalar.copy(dst, src)
-
-        def deal_rows(i, engine, lo, hi):
-            src = w_raw[i][:].rearrange("p j (l u e) -> p u l e j", u=2, e=2)[:, :, lo:hi]
-            dst = dealt[parts[i][0]][:].rearrange("p (u e) l j -> p u l e j", e=2)[:, :, lo:hi]
+            src = w_raw[i][:].rearrange("p j (l u e) -> p u l e j", u=2, e=2)[:, halves, lo:hi]
+            dst = dealt[g][:].rearrange("p (u e) l j -> p u l e j", e=2)[:, halves, lo:hi, :, rows]
             if engine == "vector":
                 nc.vector.tensor_copy(dst, src)
             else:
@@ -105,15 +97,15 @@ def tile_picked_zkvw_tanh_po_kernel(tc, x_words, x_scales, cache, w1, scale, off
 
         nc.vector.tensor_copy(sg[:], xs[:].indirect(offs_sb[:]))
         nc.vector.tensor_copy(xg[0][:], xw[0][:].indirect(offs_sb[:]))
-        deal_rows(0, "scalar", 0, 32)
-        deal_rows(0, "vector", 32, P)
+        deal(0, "scalar", 0, 32)
+        deal(0, "vector", 32, P)
         quantise(0)
         multiply(0)
         deal(1, "scalar", 0, FIRST_PAIR_ON_SCALAR)
         deal(1, "vector", FIRST_PAIR_ON_SCALAR, P)
-        deal(2, "scalar", 0, ON_SCALAR)
-        deal(3, "vector", ON_SCALAR, P, slice(0, 2))
-        deal(3, "vector", ON_SCALAR, P, slice(2, PACK))
+        for u in range(2):
+            deal(2, "scalar", 0, ON_SCALAR, slice(u, u + 1))
+            deal(2, "vector", ON_SCALAR, P, slice(u, u + 1))
         quantise(1)
         for lo, hi in ((0, S // 2), (S // 2, S)):
             nc.vector.tensor_copy(xg[1][:, lo:hi], xw[1][:].indirect(offs_sb[:, lo // LIST_ROWS : hi // LIST_ROWS]))
@@ -153,7 +145,7 @@ def tile_picked_zkvw_tanh_po_kernel(tc, x_words, x_scales, cache, w1, scale, off
         def store(t):
             nc.sync.dma_start(plane_of(out_0, t), window[t][:])
 
-        spans = ((0, 256, "vector"), (256, 512, "vector"), (512, 640, "scalar"), (640, 896, "scalar"), (896, 1024, "scalar"))
+        spans = ((0, 256, "vector"), (256, 512, "vector"), (512, 768, "scalar"), (768, 896, "scalar"), (896, 1024, "scalar"))
         joined = sb("joined", [P, 2, U, 2], BF16)
         pairs = [joined[:, :, lo:hi] for lo, hi, engine in spans]
         woven = [sb("woven%d" % c, [P, hi - lo, 2], F32) for c, (lo, hi, engine) in enumerate(spans)]
@@ -188,9 +180,8 @@ def tile_picked_zkvw_tanh_po_kernel(tc, x_words, x_scales, cache, w1, scale, off
         def quantise_span(c):
             lo, hi, engine = spans[c]
             nc.vector.quantize_mx(out=codes[:, lo:hi].bitcast(FP8X4), scales=plane[:, lo:hi], in_=woven[c][:].rearrange("p c u -> p (c u)").bitcast(BF16))
-            if c != 2:
-                since = lo
-                hi = spans[2][1] if c == 1 else hi
+            if c != 3:
+                since = spans[3][0] if c == 4 else lo
                 nc.sync.dma_start(out_words[:, since:hi], codes[:, since:hi].bitcast(I32))
 
         def put(engine, t, lo, hi):

@@ -23,7 +23,7 @@ PASSES = 2
 LIST_ROWS = 16
 BORDER = 512
 ON_SCALAR = 56
-FIRST_PAIR_ON_SCALAR = 64
+FIRST_PAIR_ON_SCALAR = 80
 
 
 def tile_picked_zkvw_tanh_po_kernel(tc, x_words, x_scales, cache, w1, scale, offs, slot, out_0, out_1, out_2):
@@ -39,7 +39,7 @@ def tile_picked_zkvw_tanh_po_kernel(tc, x_words, x_scales, cache, w1, scale, off
         slot_sb = sb("slot_sb", [P, S // LIST_ROWS], U16)
         xw = [sb("xw%d" % g, [P, T], U32) for g in range(PASSES)]
         xs = sb("xs", [P, T], U8)
-        parts = ((0, slice(0, 4), 0, P), (1, slice(0, 2), 0, P), (1, slice(2, 4), 0, P))
+        parts = tuple((g, slice(j, j + 2), 0, P) for g in range(PASSES) for j in (0, 2))
         w_raw = [sb("w_raw%d" % i, [P, rows.stop - rows.start, PACK * (hi - lo)], F32) for i, (g, rows, lo, hi) in enumerate(parts)]
         scale_sb = sb("scale_sb", [P, S], F32)
         window = [sb("window%d" % t, [P, U], F32) for t in range(PACK)]
@@ -66,7 +66,7 @@ def tile_picked_zkvw_tanh_po_kernel(tc, x_words, x_scales, cache, w1, scale, off
         load_x(1)
         nc.sync.dma_start(scale_sb[:], scale)
         nc.sync.dma_start(slot_sb[:], slot)
-        for t, lo, hi in ((0, 0, U), (1, 0, U), (2, 0, 768), (3, 0, S), (3, S, U), (2, 768, U)):
+        for t, lo, hi in ((0, 0, U), (1, 0, U), (2, 0, 768), (3, 0, U), (2, 768, U)):
             nc.sync.dma_start(window[t][:, lo:hi], plane_of(cache, t)[:, lo:hi])
 
         xg = [sb("xg%d" % g, [P, S], U32) for g in range(PASSES)]
@@ -97,15 +97,15 @@ def tile_picked_zkvw_tanh_po_kernel(tc, x_words, x_scales, cache, w1, scale, off
 
         nc.vector.tensor_copy(sg[:], xs[:].indirect(offs_sb[:]))
         nc.vector.tensor_copy(xg[0][:], xw[0][:].indirect(offs_sb[:]))
-        deal(0, "scalar", 0, 32)
-        deal(0, "vector", 32, P)
+        deal(0, "scalar", 0, P)
+        deal(1, "vector", 0, P)
         quantise(0)
         multiply(0)
-        deal(1, "scalar", 0, FIRST_PAIR_ON_SCALAR)
-        deal(1, "vector", FIRST_PAIR_ON_SCALAR, P)
+        deal(2, "scalar", 0, FIRST_PAIR_ON_SCALAR)
+        deal(2, "vector", FIRST_PAIR_ON_SCALAR, P)
         for u in range(2):
-            deal(2, "scalar", 0, ON_SCALAR, slice(u, u + 1))
-            deal(2, "vector", ON_SCALAR, P, slice(u, u + 1))
+            deal(3, "scalar", 0, ON_SCALAR, slice(u, u + 1))
+            deal(3, "vector", ON_SCALAR, P, slice(u, u + 1))
         quantise(1)
         for lo, hi in ((0, S // 2), (S // 2, S)):
             nc.vector.tensor_copy(xg[1][:, lo:hi], xw[1][:].indirect(offs_sb[:, lo // LIST_ROWS : hi // LIST_ROWS]))

@@ -22,7 +22,7 @@ PACK = 4
 PASSES = 2
 LIST_ROWS = 16
 BORDER = 512
-ON_SCALAR = 56
+ON_SCALAR = 48
 FIRST_PAIR_ON_SCALAR = 80
 
 

from contextlib import ExitStack

import concourse.mybir as mybir

K, T, S, N, U = 1024, 1024, 512, 512, 1024
FLOPS = 2 * K * N * S

F32 = mybir.dt.float32
BF16 = mybir.dt.bfloat16
I32 = mybir.dt.int32
U32 = mybir.dt.uint32
U16 = mybir.dt.uint16
U8 = mybir.dt.uint8
FP8X4 = mybir.dt.float8_e4m3fn_x4
TANH = mybir.ActivationFunctionType.Tanh
COPY = mybir.ActivationFunctionType.Copy
MULT = mybir.AluOpType.mult
ADD = mybir.AluOpType.add

P = 128
PACK = 4
PASSES = 2
LIST_ROWS = 16
BORDER = 512
ON_SCALAR = 48
FIRST_PAIR_ON_SCALAR = 80


def tile_picked_zkvw_tanh_po_kernel(tc, x_words, x_scales, cache, w1, scale, offs, slot, out_0, out_1, out_2):
    nc = tc.nc
    with ExitStack() as ctx:
        held = ctx.enter_context(tc.tile_pool(name="held", bufs=1))
        psum = ctx.enter_context(tc.psum_pool(name="psum", bufs=1))

        def sb(name, shape, dtype, tag=None):
            return held.tile(shape, dtype, name=name, tag=tag or name, align_bytes=64)

        offs_sb = sb("offs_sb", [P, S // LIST_ROWS], U16)
        slot_sb = sb("slot_sb", [P, S // LIST_ROWS], U16)
        xw = [sb("xw%d" % g, [P, T], U32) for g in range(PASSES)]
        xs = sb("xs", [P, T], U8)
        parts = tuple((g, slice(j, j + 2), 0, P) for g in range(PASSES) for j in (0, 2))
        w_raw = [sb("w_raw%d" % i, [P, rows.stop - rows.start, PACK * (hi - lo)], F32) for i, (g, rows, lo, hi) in enumerate(parts)]
        scale_sb = sb("scale_sb", [P, S], F32)
        window = [sb("window%d" % t, [P, U], F32) for t in range(PACK)]

        nc.vector.memset(xs[:].bitcast(I32), 0)

        w_rows = w1.rearrange("(g p j) n -> g p j n", g=PASSES, j=PACK)

        def load_x(g):
            nc.sync.dma_start(xw[g][:].bitcast(I32), x_words[g].rearrange("p c r -> p (c r)").bitcast(I32))

        def load_w():
            for i, (g, rows, lo, hi) in enumerate(parts):
                nc.sync.dma_start(w_raw[i][:], w_rows[g][:, rows, PACK * lo : PACK * hi])

        def plane_of(matrix, t):
            return matrix.rearrange("(l r) c -> l r c", r=PACK)[:, t, :]

        load_x(0)
        nc.sync.dma_start(offs_sb[:], offs)
        for q in range(4):
            nc.sync.dma_start(xs[32 * q : 32 * q + 8, :].bitcast(I32), x_scales[:, 4 * q : 4 * q + 4, :].bitcast(I32))
        load_w()
        load_x(1)
        nc.sync.dma_start(scale_sb[:], scale)
        nc.sync.dma_start(slot_sb[:], slot)
        for t, lo, hi in ((0, 0, U), (1, 0, U), (2, 0, 768), (3, 0, U), (2, 768, U)):
            nc.sync.dma_start(window[t][:, lo:hi], plane_of(cache, t)[:, lo:hi])

        xg = [sb("xg%d" % g, [P, S], U32) for g in range(PASSES)]
        sg = sb("sg", [P, S], U8)
        dealt = [sb("dealt%d" % g, [P, PACK, P, PACK], BF16) for g in range(PASSES)]
        w_q = [[sb("w_q%d_%d" % (g, t), [P, P], U32) for t in range(PACK)] for g in range(PASSES)]
        w_s = [[sb("w_s%d_%d" % (g, t), [P, P], U8) for t in range(PACK)] for g in range(PASSES)]
        pieces = ((1, 0, S // 2), (0, 0, S // 2), (1, S // 2, S), (0, S // 2, S), (2, 0, S), (3, 0, S // 2), (3, S // 2, S))
        sums = [psum.tile([P, hi - lo], F32, name="sums%d" % i, tag="sums%d" % i) for i, (t, lo, hi) in enumerate(pieces)]

        def deal(i, engine, lo, hi, halves=slice(0, 2)):
            g, rows, first, end = parts[i]
            src = w_raw[i][:].rearrange("p j (l u e) -> p u l e j", u=2, e=2)[:, halves, lo:hi]
            dst = dealt[g][:].rearrange("p (u e) l j -> p u l e j", e=2)[:, halves, lo:hi, :, rows]
            if engine == "vector":
                nc.vector.tensor_copy(dst, src)
            else:
                nc.scalar.copy(dst, src)

        def quantise(g):
            for t in (1, 0, 2, 3):
                nc.vector.quantize_mx(out=w_q[g][t][:].bitcast(FP8X4), scales=w_s[g][t][:], in_=dealt[g][:, t].rearrange("p l j -> p (l j)"))

        def multiply(g):
            for i in (0, 5, 1, 2, 3, 4, 6):
                t, lo, hi = pieces[i]
                nc.tensor.matmul_mx(out=sums[i][:], lhsT=w_q[g][t][:].bitcast(FP8X4), lhsT_scale=w_s[g][t][:], rhs=xg[g][:, lo:hi].bitcast(FP8X4), rhs_scale=sg[4 * g : P, lo:hi], start=g == 0, stop=g == PASSES - 1)

        nc.vector.tensor_copy(sg[:], xs[:].indirect(offs_sb[:]))
        nc.vector.tensor_copy(xg[0][:], xw[0][:].indirect(offs_sb[:]))
        deal(0, "scalar", 0, P)
        deal(1, "vector", 0, P)
        quantise(0)
        multiply(0)
        deal(2, "scalar", 0, FIRST_PAIR_ON_SCALAR)
        deal(2, "vector", FIRST_PAIR_ON_SCALAR, P)
        for u in range(2):
            deal(3, "scalar", 0, ON_SCALAR, slice(u, u + 1))
            deal(3, "vector", ON_SCALAR, P, slice(u, u + 1))
        quantise(1)
        for lo, hi in ((0, S // 2), (S // 2, S)):
            nc.vector.tensor_copy(xg[1][:, lo:hi], xw[1][:].indirect(offs_sb[:, lo // LIST_ROWS : hi // LIST_ROWS]))
        multiply(1)

        first = 3
        starts = [sum(hi - lo for t, lo, hi in pieces[first:i]) for i in range(first, len(pieces) + 1)]
        scaled_late = sb("scaled_late", [P, starts[-1]], F32)
        scaled = [sb("scaled%d" % i, [P, S // 2], F32)[:] for i in range(first)]
        scaled += [scaled_late[:, lo:hi] for lo, hi in zip(starts, starts[1:])]
        moved = sb("moved", [P, S // 2], F32)
        nc.scalar.copy(moved[:], sums[5][:])
        for i, (t, lo, hi) in enumerate(pieces):
            if i == 5:
                nc.gpsimd.tensor_tensor(scaled[i], moved[:], scale_sb[:, lo:hi], MULT)
            else:
                nc.vector.tensor_tensor(scaled[i], sums[i][:], scale_sb[:, lo:hi], MULT)

        early = sb("early", [P, S // 2], F32)
        whole = sb("whole", [P, S], F32)
        late = sb("late", [P, starts[-1]], F32, "scale_sb")

        def bounded(t, lo, hi):
            if t == 1:
                return whole[:, lo:hi]
            if t == 0:
                return early[:, lo:hi] if hi <= S // 2 else late[:, lo - S // 2 : hi - S // 2]
            return late[:, starts[t - 1] + lo : starts[t - 1] + hi]

        def scatter(engine, t, lo, hi):
            target = window[t][:].indirect(slot_sb[:, lo // LIST_ROWS : hi // LIST_ROWS])
            if engine == "vector":
                nc.vector.tensor_copy(target, bounded(t, lo, hi))
            else:
                nc.scalar.activation(target, bounded(t, lo, hi), COPY)

        def store(t):
            nc.sync.dma_start(plane_of(out_0, t), window[t][:])

        spans = ((0, 256, "vector"), (256, 512, "vector"), (512, 768, "scalar"), (768, 896, "scalar"), (896, 1024, "scalar"))
        joined = sb("joined", [P, 2, U, 2], BF16)
        pairs = [joined[:, :, lo:hi] for lo, hi, engine in spans]
        woven = [sb("woven%d" % c, [P, hi - lo, 2], F32) for c, (lo, hi, engine) in enumerate(spans)]

        def weave(c):
            src = pairs[c].rearrange("p u c e -> p u (c e)").bitcast(F32).rearrange("p u c -> p c u")
            if spans[c][2] == "vector":
                nc.vector.tensor_copy(woven[c][:], src)
            else:
                nc.scalar.copy(woven[c][:], src)

        for i in range(first):
            nc.scalar.activation(bounded(*pieces[i]), scaled[i], TANH)
        scatter("scalar", 0, 0, S // 2)
        scatter("vector", 1, 0, S)
        nc.scalar.activation(late[:, 0 : starts[1]], scaled_late[:, 0 : starts[1]], TANH)
        nc.scalar.activation(late[:, starts[1] :], scaled_late[:, starts[1] :], TANH)
        scatter("scalar", 0, S // 2, S)
        store(1)
        store(0)
        for t in (1, 0):
            nc.gpsimd.tensor_scalar(joined[:, 0, :, t], window[t][:], 1.0, -0.0, MULT, ADD)
        scatter("vector", 3, 0, 128)
        scatter("vector", 2, 0, S)
        scatter("scalar", 3, 128, S)
        store(3)
        store(2)
        codes = sb("codes", [P, U], U32)
        plane = sb("plane", [P, U], U8)
        out_words = out_1[0].rearrange("p c r -> p (c r)").bitcast(I32)

        def quantise_span(c):
            lo, hi, engine = spans[c]
            nc.vector.quantize_mx(out=codes[:, lo:hi].bitcast(FP8X4), scales=plane[:, lo:hi], in_=woven[c][:].rearrange("p c u -> p (c u)").bitcast(BF16))
            if c != 3:
                since = spans[3][0] if c == 4 else lo
                nc.sync.dma_start(out_words[:, since:hi], codes[:, since:hi].bitcast(I32))

        def put(engine, t, lo, hi):
            dst, src = joined[:, 1, lo:hi, t % 2], window[t][:, lo:hi]
            if engine == "vector":
                nc.vector.tensor_copy(dst, src)
            else:
                nc.scalar.copy(dst, src)

        put("scalar", 3, BORDER, U)
        put("scalar", 2, *spans[2][:2])
        put("scalar", 2, *spans[3][:2])
        weave(2)
        put("scalar", 2, *spans[4][:2])
        weave(3)
        weave(4)
        put("vector", 3, *spans[0][:2])
        put("vector", 2, *spans[0][:2])
        put("vector", 3, *spans[1][:2])
        weave(0)
        put("vector", 2, *spans[1][:2])
        quantise_span(0)
        weave(1)
        for c in (2, 1, 3, 4):
            quantise_span(c)
        for q in range(4):
            queue = nc.sync if q == 0 else nc.scalar
            queue.dma_start(out_2[0, 4 * q : 4 * q + 4, :].bitcast(I32), plane[32 * q : 32 * q + 4, :].bitcast(I32))
